import numpy as np
import ml_dtypes


def mxq(x, axis, fmt="e4m3"):
    dtype, down = {"e4m3": (ml_dtypes.float8_e4m3fn, 7), "e5m2": (ml_dtypes.float8_e5m2, 14)}[fmt]
    v = np.moveaxis(np.asarray(x, np.float32).astype(ml_dtypes.bfloat16).astype(np.float64), axis, -1)
    blocks = v.reshape(v.shape[:-1] + (-1, 32))
    amax = np.abs(blocks).max(-1, keepdims=True)
    byte = np.maximum(np.where(amax > 0, np.frexp(amax)[1] - 1 + 127, 0) - down, 1)
    scale = np.exp2(byte - 127.0)
    codes = (blocks / scale).astype(np.float32).astype(dtype).astype(np.float64)
    return np.moveaxis((codes * scale).reshape(v.shape), -1, axis)


WIDE = False


def mx_kscale(k):
    if not WIDE:
        return np.ones(k)
    levels = np.array([10, -10, 5, -5, 0])
    if k % 512:
        return np.exp2(np.random.permutation(np.resize(levels, k // 32))).repeat(32)
    a = np.empty((k // 512, 16))
    for p in range(k // 512):
        a[p, :8] = np.random.permutation(np.resize(levels, 8))
        for g in range(8):
            far = levels[np.abs(levels - a[p, g]) >= 10]
            a[p, g + 8] = far[np.random.randint(len(far))]
    return np.exp2(a.ravel()).repeat(32)


def f64(x):
    return np.asarray(x).astype(np.float64)


E2M1 = np.array([0.0, 0.5, 1.0, 1.5, 2.0, 3.0, 4.0, 6.0, -0.0, -0.5, -1.0, -1.5, -2.0, -3.0, -4.0, -6.0])


def pack_weight(w, fmt):
    k, n = w.shape
    w = f64(np.asarray(w, np.float32).astype(ml_dtypes.bfloat16)).reshape(k // 32, 32, n)
    amax = np.abs(w).max(1)
    if fmt == "e4m3":
        byte = np.frexp(amax)[1] - 1 + 127 - 7
    else:
        mant, ex = np.frexp(amax / 6.0)
        byte = np.where(mant > 0.5, ex, ex - 1) + 127
    byte = np.clip(np.where(amax > 0, byte, 1), 1, 254)
    scaled = (w * np.exp2(127.0 - byte)[:, None, :]).reshape(k, n).astype(np.float32)
    by_word = np.ascontiguousarray(scaled.reshape(k // 512, 128, 4, n).transpose(0, 1, 3, 2))
    if fmt == "e4m3":
        words = by_word.astype(ml_dtypes.float8_e4m3fn).view(np.uint8)
    else:
        c = by_word.astype(ml_dtypes.float4_e2m1fn).view(np.uint8) & 0xF
        words = (c[..., 0::2] | (c[..., 1::2] << 4)).reshape(k // 512, 128, 2 * n)
    return np.ascontiguousarray(words), np.ascontiguousarray(byte.astype(np.uint8).reshape(k // 512, 16, n))


def unpack_weight(words, scales, fmt):
    g, _, n = scales.shape
    words = np.ascontiguousarray(words).reshape(g, 128, n, -1)
    if fmt == "e4m3":
        vals = words.view(ml_dtypes.float8_e4m3fn).astype(np.float64)
    else:
        nib = np.empty((g, 128, n, 4), np.uint8)
        nib[..., 0::2] = words & 0xF
        nib[..., 1::2] = words >> 4
        vals = E2M1[nib]
    vals = vals * np.repeat(np.exp2(scales.astype(np.float64) - 127.0), 8, axis=1)[..., None]
    return vals.transpose(0, 1, 3, 2).reshape(g * 512, n)


def silu(v):
    return v / (1.0 + np.exp(-np.maximum(v, -700.0)))


K, M, T = 512, 1024, 1536


def setup_inputs():
    n = np.random.standard_normal
    s = mx_kscale(K)[:, None]
    p_w4 = pack_weight(n((K, M)) / np.sqrt(K) / s ** 2, "e2m1")
    p_w8 = pack_weight(n((K, M)) / np.sqrt(K) / s, "e4m3")
    return {
        "x": (n((K, T)) * s).astype(np.float32),
        "w4_words": p_w4[0],
        "w4_scales": p_w4[1],
        "w8_words": p_w8[0],
        "w8_scales": p_w8[1],
        "b": (0.3 * n(1024)).astype(np.float32),
    }


def reference(x, w4_words, w4_scales, w8_words, w8_scales, b):
    xa_, xb_ = mxq(f64(x) ** 2, 0, "e4m3"), mxq(f64(x), 0, "e4m3")
    w4_ = unpack_weight(w4_words, w4_scales, "e2m1")
    w8_ = unpack_weight(w8_words, w8_scales, "e4m3")
    y = xa_.T @ w4_ + xb_.T @ w8_
    return silu(y + f64(b)[None, :])

@@ -1,0 +1,208 @@
+from contextlib import ExitStack
+
+import concourse.mybir as mybir
+from concourse.masks import make_identity
+
+K, M, T = 512, 1024, 1536
+FLOPS = 2 * 2 * K * M * T
+
+F32 = mybir.dt.float32
+BF16 = mybir.dt.bfloat16
+I32 = mybir.dt.int32
+U32 = mybir.dt.uint32
+U8 = mybir.dt.uint8
+FP8X4 = mybir.dt.float8_e4m3fn_x4
+FP4X4 = mybir.dt.float4_e2m1fn_x4
+ACT = mybir.ActivationFunctionType
+ALU = mybir.AluOpType
+
+P = 128
+PACK = 4
+BANK = 512
+LOADS = [256, 256, 256, 256, 512]
+CHUNKS = [128, 128, 256, 256, 256, 256, 256]
+
+
+def tile_mix_feat_tm_quad_silu_kernel(tc, x, w4_words, w4_scales, w8_words, w8_scales, b, out):
+    nc = tc.nc
+    with ExitStack() as ctx:
+        keep = ctx.enter_context(tc.tile_pool(name="keep", bufs=1))
+        pre_pool = ctx.enter_context(tc.tile_pool(name="pre", bufs=4))
+        psum = ctx.enter_context(tc.psum_pool(name="psum", bufs=8))
+        ctx.enter_context(tc.manual_schedule())
+
+        w8 = keep.tile([P, M], U32, name="w8", align_bytes=64)
+        w4 = keep.tile([P, 2 * M], U8, name="w4", align_bytes=64)
+        planes = keep.tile([P, 2, M], U8, name="planes", align_bytes=64)
+        b_cols = keep.tile([P, 2, 8], F32, name="b_cols")
+        ident = keep.tile([P, P], F32, name="ident")
+        bias = keep.tile([P, M], F32, name="bias")
+        warm = keep.tile([P, 8], F32, name="warm")
+        warm_out = keep.tile([P, 8], F32, name="warm_out")
+
+        load_start = [sum(LOADS[:i]) for i in range(len(LOADS))]
+        raw = [keep.tile([P, PACK, w], F32, name="raw%d" % i) for i, w in enumerate(LOADS)]
+        chunk_start = [sum(CHUNKS[:c]) for c in range(len(CHUNKS))]
+        feats = [keep.tile([P, 2, w, PACK], BF16, name="feats%d" % c, align_bytes=64) for c, w in enumerate(CHUNKS)]
+        codes = [keep.tile([P, 2, w], U32, name="codes%d" % c, align_bytes=64) for c, w in enumerate(CHUNKS)]
+        scales = [keep.tile([P, 2, w], U8, name="scales%d" % c, align_bytes=64) for c, w in enumerate(CHUNKS)]
+        res = [keep.tile([P, M], F32, name="res%d" % i) for i in range(T // P)]
+        acc = {}
+        pre = {}
+
+        x_rows = x.rearrange("(p j) t -> p j t", j=PACK)
+        w8_src = w8_words[0].rearrange("p n i -> p (n i)").bitcast(I32)
+
+        def load_x(i):
+            nc.sync.dma_start(out=raw[i][:], in_=x_rows[:, :, load_start[i] : load_start[i] + LOADS[i]])
+
+        def load_scales(which, src):
+            for q in range(4):
+                nc.sync.dma_start(
+                    out=planes[32 * q : 32 * q + 4, which, :].bitcast(I32),
+                    in_=src[0, 4 * q : 4 * q + 4, :].bitcast(I32),
+                )
+
+        def load_w8(h):
+            nc.sync.dma_start(out=w8[:, h * BANK : (h + 1) * BANK].bitcast(I32), in_=w8_src[:, h * BANK : (h + 1) * BANK])
+
+        def raw_view(c):
+            i = max(j for j in range(len(LOADS)) if load_start[j] <= chunk_start[c])
+            t0 = chunk_start[c] - load_start[i]
+            return raw[i][:, :, t0 : t0 + CHUNKS[c]].rearrange("p j (g i) -> p g j i", i=4)
+
+        def feat_view(c, which):
+            return feats[c][:, which, :, :].rearrange("p (g i) j -> p g j i", i=4)
+
+        def cast(c):
+            nc.vector.tensor_copy(out=feat_view(c, 0), in_=raw_view(c))
+
+        def square(c):
+            nc.scalar.activation(out=feat_view(c, 1), in_=raw_view(c), func=ACT.Square)
+
+        def quantize(c):
+            nc.vector.quantize_mx(
+                out=codes[c][:].rearrange("p f t -> p (f t)").bitcast(FP8X4),
+                scales=scales[c][:].rearrange("p f t -> p (f t)"),
+                in_=feats[c][:].rearrange("p f t j -> p (f t j)"),
+            )
+
+        def multiply(i, h):
+            c = max(j for j in range(len(CHUNKS)) if chunk_start[j] <= i * P)
+            cols = slice(i * P - chunk_start[c], i * P - chunk_start[c] + P)
+            n = slice(h * BANK, (h + 1) * BANK)
+            acc[i, h] = psum.tile([P, BANK], F32, name="acc")
+            nc.tensor.matmul_mx(
+                out=acc[i, h][:],
+                lhsT=codes[c][:, 0, cols].bitcast(FP8X4),
+                lhsT_scale=scales[c][:, 0, cols],
+                rhs=w8[:, n].bitcast(FP8X4),
+                rhs_scale=planes[:, 0, n],
+                start=True,
+                stop=False,
+            )
+            nc.tensor.matmul_mx(
+                out=acc[i, h][:],
+                lhsT=codes[c][:, 1, cols].bitcast(FP8X4),
+                lhsT_scale=scales[c][:, 1, cols],
+                rhs=w4[:, 2 * h * BANK : 2 * (h + 1) * BANK].bitcast(FP4X4),
+                rhs_scale=planes[:, 1, n],
+                start=False,
+                stop=True,
+            )
+
+        def add_bias(i, h):
+            if i not in pre:
+                pre[i] = pre_pool.tile([P, M], F32, name="pre")
+            n = slice(h * BANK, (h + 1) * BANK)
+            nc.vector.tensor_tensor(out=pre[i][:, n], in0=acc[i, h][:], in1=bias[:, n], op=ALU.add)
+
+        def silu(i, n):
+            nc.scalar.activation(out=res[i][:, n], in_=pre[i][:, n], func=ACT.Silu)
+
+        def store(i, n):
+            nc.sync.dma_start(out=out[i * P : (i + 1) * P, n], in_=res[i][:, n])
+
+        lo, hi, both = slice(0, BANK), slice(BANK, M), slice(0, M)
+
+        nc.vector.memset(planes[:].rearrange("p f n -> p (f n)").bitcast(I32), 0)
+        nc.gpsimd.memset(warm[:], 0.0)
+        load_x(0)
+        nc.scalar.dma_start(out=b_cols[:, :, 0:PACK], in_=b.rearrange("(h p c) -> p h c", h=2, c=PACK))
+        nc.scalar.activation(out=warm_out[:], in_=warm[:], func=ACT.Silu)
+        make_identity(nc, ident[:])
+        load_scales(0, w8_scales)
+        nc.sync.dma_start(out=w4[:].bitcast(I32), in_=w4_words[0].bitcast(I32))
+        load_w8(0)
+        load_scales(1, w4_scales)
+        load_w8(1)
+        for i in range(1, len(LOADS)):
+            load_x(i)
+
+        spread = []
+        for h in range(2):
+            bank = psum.tile([P, BANK], F32, name="acc")
+            for c in range(PACK):
+                nc.tensor.transpose(bank[:, c * P : (c + 1) * P], b_cols[:, h, c : c + 1].to_broadcast([P, P]), ident[:])
+            spread.append(bank)
+
+        def bias_views(h):
+            return (
+                bias[:, h * BANK : (h + 1) * BANK].rearrange("q (p c) -> q p c", c=PACK),
+                spread[h][:].rearrange("q (c p) -> q p c", c=PACK),
+            )
+
+        cast(0)
+        square(0)
+        quantize(0)
+        cast(1)
+        square(1)
+        nc.vector.tensor_copy(*bias_views(0))
+        nc.scalar.copy(*bias_views(1))
+        quantize(1)
+        multiply(0, 0)
+        multiply(1, 0)
+        multiply(0, 1)
+        multiply(1, 1)
+        add_bias(0, 0)
+        silu(0, lo)
+        add_bias(1, 0)
+        square(2)
+        cast(2)
+        silu(1, lo)
+        add_bias(0, 1)
+        quantize(2)
+        silu(0, hi)
+        store(0, both)
+        square(3)
+        add_bias(1, 1)
+        silu(1, hi)
+        store(1, both)
+
+        last = len(CHUNKS) - 1
+        for c in range(2, last + 1):
+            i = chunk_start[c] // P
+            for step in range(2):
+                multiply(i + step, 0)
+                multiply(i + step, 1)
+            if c < last:
+                cast(c + 1)
+            add_bias(i, 0)
+            add_bias(i, 1)
+            if c < last:
+                quantize(c + 1)
+            silu(i, both)
+            store(i, both)
+            if c + 2 <= last:
+                square(c + 2)
+            add_bias(i + 1, 0)
+            if c == last:
+                silu(i + 1, lo)
+                store(i + 1, lo)
+            add_bias(i + 1, 1)
+            if c == last:
+                silu(i + 1, hi)
+                store(i + 1, hi)
+            else:
+                silu(i + 1, both)
+                store(i + 1, both)

@@ -69,10 +69,10 @@ def tile_mix_feat_tm_quad_silu_kernel(tc, x, w4_words, w4_scales, w8_words, w8_s
         def raw_view(c):
             i = max(j for j in range(len(LOADS)) if load_start[j] <= chunk_start[c])
             t0 = chunk_start[c] - load_start[i]
-            return raw[i][:, :, t0 : t0 + CHUNKS[c]].rearrange("p j (g i) -> p g j i", i=4)
+            return raw[i][:, :, t0 : t0 + CHUNKS[c]].rearrange("p j (g i) -> p g j i", i=2)
 
         def feat_view(c, which):
-            return feats[c][:, which, :, :].rearrange("p (g i) j -> p g j i", i=4)
+            return feats[c][:, which, :, :].rearrange("p (g i) j -> p g j i", i=2)
 
         def cast(c):
             nc.vector.tensor_copy(out=feat_view(c, 0), in_=raw_view(c))

@@ -19,8 +19,11 @@ ALU = mybir.AluOpType
 P = 128
 PACK = 4
 BANK = 512
+RUN = 2
 LOADS = [256, 256, 256, 256, 512]
 CHUNKS = [128, 128, 256, 256, 256, 256, 256]
+FIRST_SHARED = 2
+VECTOR_SQUARES = 32
 
 
 def tile_mix_feat_tm_quad_silu_kernel(tc, x, w4_words, w4_scales, w8_words, w8_scales, b, out):
@@ -43,7 +46,10 @@ def tile_mix_feat_tm_quad_silu_kernel(tc, x, w4_words, w4_scales, w8_words, w8_s
         load_start = [sum(LOADS[:i]) for i in range(len(LOADS))]
         raw = [keep.tile([P, PACK, w], F32, name="raw%d" % i) for i, w in enumerate(LOADS)]
         chunk_start = [sum(CHUNKS[:c]) for c in range(len(CHUNKS))]
-        feats = [keep.tile([P, 2, w, PACK], BF16, name="feats%d" % c, align_bytes=64) for c, w in enumerate(CHUNKS)]
+        head_feats = [
+            keep.tile([P, 2, CHUNKS[c], PACK], BF16, name="feats%d" % c, align_bytes=64) for c in range(FIRST_SHARED)
+        ]
+        shared = keep.tile([P, 3, CHUNKS[FIRST_SHARED], PACK], BF16, name="shared", align_bytes=64)
         codes = [keep.tile([P, 2, w], U32, name="codes%d" % c, align_bytes=64) for c, w in enumerate(CHUNKS)]
         scales = [keep.tile([P, 2, w], U8, name="scales%d" % c, align_bytes=64) for c, w in enumerate(CHUNKS)]
         res = [keep.tile([P, M], F32, name="res%d" % i) for i in range(T // P)]
@@ -63,39 +69,66 @@ def tile_mix_feat_tm_quad_silu_kernel(tc, x, w4_words, w4_scales, w8_words, w8_s
                     in_=src[0, 4 * q : 4 * q + 4, :].bitcast(I32),
                 )
 
-        def load_w8(h):
-            nc.sync.dma_start(out=w8[:, h * BANK : (h + 1) * BANK].bitcast(I32), in_=w8_src[:, h * BANK : (h + 1) * BANK])
+        def feats(c):
+            if c < FIRST_SHARED:
+                return head_feats[c][:]
+            return shared[:, c % 2 : c % 2 + 2, :, :]
 
-        def raw_view(c):
+        def linear_slot(c):
+            return 1 - c % 2
+
+        def raw_rows(c):
             i = max(j for j in range(len(LOADS)) if load_start[j] <= chunk_start[c])
             t0 = chunk_start[c] - load_start[i]
-            return raw[i][:, :, t0 : t0 + CHUNKS[c]].rearrange("p j (g i) -> p g j i", i=2)
+            return raw[i][:, :, t0 : t0 + CHUNKS[c]]
 
-        def feat_view(c, which):
-            return feats[c][:, which, :, :].rearrange("p (g i) j -> p g j i", i=2)
+        def raw_view(c, lo, hi):
+            return raw_rows(c)[:, :, lo:hi].rearrange("p j (g i) -> p g j i", i=RUN)
+
+        def feat_view(c, slot, lo, hi):
+            return feats(c)[:, slot, lo:hi, :].rearrange("p (g i) j -> p g j i", i=RUN)
 
         def cast(c):
-            nc.vector.tensor_copy(out=feat_view(c, 0), in_=raw_view(c))
+            nc.vector.tensor_copy(out=feat_view(c, linear_slot(c), 0, CHUNKS[c]), in_=raw_view(c, 0, CHUNKS[c]))
 
-        def square(c):
-            nc.scalar.activation(out=feat_view(c, 1), in_=raw_view(c), func=ACT.Square)
+        def cast_gpsimd(c):
+            nc.gpsimd.tensor_scalar(
+                out=feats(c)[:, linear_slot(c), :, :],
+                in0=raw_rows(c).rearrange("p j t -> p t j"),
+                scalar1=1.0,
+                scalar2=0.0,
+                op0=ALU.mult,
+                op1=ALU.add,
+            )
+
+        def square(c, lo=0):
+            nc.scalar.activation(
+                out=feat_view(c, 1 - linear_slot(c), lo, CHUNKS[c]), in_=raw_view(c, lo, CHUNKS[c]), func=ACT.Square
+            )
+
+        def square_vector(c):
+            src = raw_view(c, 0, VECTOR_SQUARES)
+            nc.vector.tensor_tensor(
+                out=feat_view(c, 1 - linear_slot(c), 0, VECTOR_SQUARES), in0=src, in1=src, op=ALU.mult
+            )
 
         def quantize(c):
             nc.vector.quantize_mx(
                 out=codes[c][:].rearrange("p f t -> p (f t)").bitcast(FP8X4),
                 scales=scales[c][:].rearrange("p f t -> p (f t)"),
-                in_=feats[c][:].rearrange("p f t j -> p (f t j)"),
+                in_=feats(c).rearrange("p f t j -> p (f t j)"),
             )
 
         def multiply(i, h):
             c = max(j for j in range(len(CHUNKS)) if chunk_start[j] <= i * P)
             cols = slice(i * P - chunk_start[c], i * P - chunk_start[c] + P)
             n = slice(h * BANK, (h + 1) * BANK)
+            lin = linear_slot(c)
             acc[i, h] = psum.tile([P, BANK], F32, name="acc")
             nc.tensor.matmul_mx(
                 out=acc[i, h][:],
-                lhsT=codes[c][:, 0, cols].bitcast(FP8X4),
-                lhsT_scale=scales[c][:, 0, cols],
+                lhsT=codes[c][:, lin, cols].bitcast(FP8X4),
+                lhsT_scale=scales[c][:, lin, cols],
                 rhs=w8[:, n].bitcast(FP8X4),
                 rhs_scale=planes[:, 0, n],
                 start=True,
@@ -103,39 +136,48 @@ def tile_mix_feat_tm_quad_silu_kernel(tc, x, w4_words, w4_scales, w8_words, w8_s
             )
             nc.tensor.matmul_mx(
                 out=acc[i, h][:],
-                lhsT=codes[c][:, 1, cols].bitcast(FP8X4),
-                lhsT_scale=scales[c][:, 1, cols],
+                lhsT=codes[c][:, 1 - lin, cols].bitcast(FP8X4),
+                lhsT_scale=scales[c][:, 1 - lin, cols],
                 rhs=w4[:, 2 * h * BANK : 2 * (h + 1) * BANK].bitcast(FP4X4),
                 rhs_scale=planes[:, 1, n],
                 start=False,
                 stop=True,
             )
 
-        def add_bias(i, h):
+        def add_bias(i, lo, hi):
             if i not in pre:
                 pre[i] = pre_pool.tile([P, M], F32, name="pre")
-            n = slice(h * BANK, (h + 1) * BANK)
-            nc.vector.tensor_tensor(out=pre[i][:, n], in0=acc[i, h][:], in1=bias[:, n], op=ALU.add)
+            h = lo // BANK
+            nc.vector.tensor_tensor(
+                out=pre[i][:, lo:hi], in0=acc[i, h][:, lo - h * BANK : hi - h * BANK], in1=bias[:, lo:hi], op=ALU.add
+            )
 
-        def silu(i, n):
-            nc.scalar.activation(out=res[i][:, n], in_=pre[i][:, n], func=ACT.Silu)
+        def silu(i, lo, hi):
+            nc.scalar.activation(out=res[i][:, lo:hi], in_=pre[i][:, lo:hi], func=ACT.Silu)
 
-        def store(i, n):
-            nc.sync.dma_start(out=out[i * P : (i + 1) * P, n], in_=res[i][:, n])
+        def store(i, lo, hi):
+            nc.sync.dma_start(out=out[i * P : (i + 1) * P, lo:hi], in_=res[i][:, lo:hi])
 
-        lo, hi, both = slice(0, BANK), slice(BANK, M), slice(0, M)
+        def finish(i, lo, hi):
+            silu(i, lo, hi)
+            store(i, lo, hi)
+
+        def finish_by_banks(i):
+            for lo, hi in [(0, BANK), (BANK, M)]:
+                add_bias(i, lo, hi)
+                silu(i, lo, hi)
+            store(i, 0, M)
 
         nc.vector.memset(planes[:].rearrange("p f n -> p (f n)").bitcast(I32), 0)
         nc.gpsimd.memset(warm[:], 0.0)
+        nc.sync.dma_start(out=b_cols[:, :, 0:PACK], in_=b.rearrange("(h p c) -> p h c", h=2, c=PACK))
         load_x(0)
-        nc.scalar.dma_start(out=b_cols[:, :, 0:PACK], in_=b.rearrange("(h p c) -> p h c", h=2, c=PACK))
         nc.scalar.activation(out=warm_out[:], in_=warm[:], func=ACT.Silu)
         make_identity(nc, ident[:])
         load_scales(0, w8_scales)
+        nc.sync.dma_start(out=w8[:].bitcast(I32), in_=w8_src)
         nc.sync.dma_start(out=w4[:].bitcast(I32), in_=w4_words[0].bitcast(I32))
-        load_w8(0)
         load_scales(1, w4_scales)
-        load_w8(1)
         for i in range(1, len(LOADS)):
             load_x(i)
 
@@ -154,55 +196,54 @@ def tile_mix_feat_tm_quad_silu_kernel(tc, x, w4_words, w4_scales, w8_words, w8_s
 
         cast(0)
         square(0)
-        quantize(0)
         cast(1)
         square(1)
+        quantize(0)
+        quantize(1)
         nc.vector.tensor_copy(*bias_views(0))
         nc.scalar.copy(*bias_views(1))
-        quantize(1)
-        multiply(0, 0)
-        multiply(1, 0)
-        multiply(0, 1)
-        multiply(1, 1)
-        add_bias(0, 0)
-        silu(0, lo)
-        add_bias(1, 0)
+        for i in range(2):
+            for h in range(2):
+                multiply(i, h)
+        add_bias(0, 0, BANK)
         square(2)
         cast(2)
-        silu(1, lo)
-        add_bias(0, 1)
+        add_bias(0, BANK, M)
         quantize(2)
-        silu(0, hi)
-        store(0, both)
+        cast_gpsimd(3)
+        finish(0, 0, M)
         square(3)
-        add_bias(1, 1)
-        silu(1, hi)
-        store(1, both)
+        add_bias(1, 0, BANK)
+        add_bias(1, BANK, M)
+        finish(1, 0, M)
 
         last = len(CHUNKS) - 1
-        for c in range(2, last + 1):
+        for c in range(FIRST_SHARED, last):
             i = chunk_start[c] // P
             for step in range(2):
-                multiply(i + step, 0)
-                multiply(i + step, 1)
-            if c < last:
-                cast(c + 1)
-            add_bias(i, 0)
-            add_bias(i, 1)
-            if c < last:
-                quantize(c + 1)
-            silu(i, both)
-            store(i, both)
+                for h in range(2):
+                    multiply(i + step, h)
+            add_bias(i, 0, BANK)
+            add_bias(i, BANK, M)
             if c + 2 <= last:
-                square(c + 2)
-            add_bias(i + 1, 0)
-            if c == last:
-                silu(i + 1, lo)
-                store(i + 1, lo)
-            add_bias(i + 1, 1)
-            if c == last:
-                silu(i + 1, hi)
-                store(i + 1, hi)
+                square_vector(c + 2)
+            quantize(c + 1)
+            finish(i, 0, M)
+            if c + 2 <= last:
+                cast_gpsimd(c + 2)
+                square(c + 2, VECTOR_SQUARES)
+            if c + 2 <= last:
+                add_bias(i + 1, 0, BANK)
+                add_bias(i + 1, BANK, M)
+                finish(i + 1, 0, M)
             else:
-                silu(i + 1, both)
-                store(i + 1, both)
+                finish_by_banks(i + 1)
+
+        i = chunk_start[last] // P
+        for step in range(2):
+            for h in range(2):
+                multiply(i + step, h)
+        finish_by_banks(i)
+        for lo, hi in [(0, BANK), (BANK, BANK + BANK // 2), (BANK + BANK // 2, M)]:
+            add_bias(i + 1, lo, hi)
+            finish(i + 1, lo, hi)

@@ -23,7 +23,7 @@ RUN = 2
 LOADS = [256, 256, 256, 256, 512]
 CHUNKS = [128, 128, 256, 256, 256, 256, 256]
 FIRST_SHARED = 2
-VECTOR_SQUARES = 32
+VECTOR_SQUARES = 64
 
 
 def tile_mix_feat_tm_quad_silu_kernel(tc, x, w4_words, w4_scales, w8_words, w8_scales, b, out):
@@ -34,8 +34,8 @@ def tile_mix_feat_tm_quad_silu_kernel(tc, x, w4_words, w4_scales, w8_words, w8_s
         psum = ctx.enter_context(tc.psum_pool(name="psum", bufs=8))
         ctx.enter_context(tc.manual_schedule())
 
-        w8 = keep.tile([P, M], U32, name="w8", align_bytes=64)
-        w4 = keep.tile([P, 2 * M], U8, name="w4", align_bytes=64)
+        w8 = [keep.tile([P, BANK], U32, name="w8_%d" % h, align_bytes=64) for h in range(2)]
+        w4 = [keep.tile([P, 2 * BANK], U8, name="w4_%d" % h, align_bytes=64) for h in range(2)]
         planes = keep.tile([P, 2, M], U8, name="planes", align_bytes=64)
         b_cols = keep.tile([P, 2, 8], F32, name="b_cols")
         ident = keep.tile([P, P], F32, name="ident")
@@ -59,6 +59,8 @@ def tile_mix_feat_tm_quad_silu_kernel(tc, x, w4_words, w4_scales, w8_words, w8_s
         x_rows = x.rearrange("(p j) t -> p j t", j=PACK)
         w8_src = w8_words[0].rearrange("p n i -> p (n i)").bitcast(I32)
 
+        w4_src = w4_words[0].bitcast(I32)
+
         def load_x(i):
             nc.sync.dma_start(out=raw[i][:], in_=x_rows[:, :, load_start[i] : load_start[i] + LOADS[i]])
 
@@ -68,6 +70,12 @@ def tile_mix_feat_tm_quad_silu_kernel(tc, x, w4_words, w4_scales, w8_words, w8_s
                     out=planes[32 * q : 32 * q + 4, which, :].bitcast(I32),
                     in_=src[0, 4 * q : 4 * q + 4, :].bitcast(I32),
                 )
+
+        def load_w8(h):
+            nc.sync.dma_start(out=w8[h][:].bitcast(I32), in_=w8_src[:, h * BANK : (h + 1) * BANK])
+
+        def load_w4(h):
+            nc.sync.dma_start(out=w4[h][:].bitcast(I32), in_=w4_src[:, h * BANK // 2 : (h + 1) * BANK // 2])
 
         def feats(c):
             if c < FIRST_SHARED:
@@ -119,9 +127,12 @@ def tile_mix_feat_tm_quad_silu_kernel(tc, x, w4_words, w4_scales, w8_words, w8_s
                 in_=feats(c).rearrange("p f t j -> p (f t j)"),
             )
 
-        def multiply(i, h):
+        def token_cols(i):
             c = max(j for j in range(len(CHUNKS)) if chunk_start[j] <= i * P)
-            cols = slice(i * P - chunk_start[c], i * P - chunk_start[c] + P)
+            return c, slice(i * P - chunk_start[c], i * P - chunk_start[c] + P)
+
+        def linear_pass(i, h):
+            c, cols = token_cols(i)
             n = slice(h * BANK, (h + 1) * BANK)
             lin = linear_slot(c)
             acc[i, h] = psum.tile([P, BANK], F32, name="acc")
@@ -129,20 +140,29 @@ def tile_mix_feat_tm_quad_silu_kernel(tc, x, w4_words, w4_scales, w8_words, w8_s
                 out=acc[i, h][:],
                 lhsT=codes[c][:, lin, cols].bitcast(FP8X4),
                 lhsT_scale=scales[c][:, lin, cols],
-                rhs=w8[:, n].bitcast(FP8X4),
+                rhs=w8[h][:].bitcast(FP8X4),
                 rhs_scale=planes[:, 0, n],
                 start=True,
                 stop=False,
             )
+
+        def square_pass(i, h):
+            c, cols = token_cols(i)
+            n = slice(h * BANK, (h + 1) * BANK)
+            lin = linear_slot(c)
             nc.tensor.matmul_mx(
                 out=acc[i, h][:],
                 lhsT=codes[c][:, 1 - lin, cols].bitcast(FP8X4),
                 lhsT_scale=scales[c][:, 1 - lin, cols],
-                rhs=w4[:, 2 * h * BANK : 2 * (h + 1) * BANK].bitcast(FP4X4),
+                rhs=w4[h][:].bitcast(FP4X4),
                 rhs_scale=planes[:, 1, n],
                 start=False,
                 stop=True,
             )
+
+        def multiply(i, h):
+            linear_pass(i, h)
+            square_pass(i, h)
 
         def add_bias(i, lo, hi):
             if i not in pre:
@@ -165,8 +185,7 @@ def tile_mix_feat_tm_quad_silu_kernel(tc, x, w4_words, w4_scales, w8_words, w8_s
         def finish_by_banks(i):
             for lo, hi in [(0, BANK), (BANK, M)]:
                 add_bias(i, lo, hi)
-                silu(i, lo, hi)
-            store(i, 0, M)
+                finish(i, lo, hi)
 
         nc.vector.memset(planes[:].rearrange("p f n -> p (f n)").bitcast(I32), 0)
         nc.gpsimd.memset(warm[:], 0.0)
@@ -175,10 +194,13 @@ def tile_mix_feat_tm_quad_silu_kernel(tc, x, w4_words, w4_scales, w8_words, w8_s
         nc.scalar.activation(out=warm_out[:], in_=warm[:], func=ACT.Silu)
         make_identity(nc, ident[:])
         load_scales(0, w8_scales)
-        nc.sync.dma_start(out=w8[:].bitcast(I32), in_=w8_src)
-        nc.sync.dma_start(out=w4[:].bitcast(I32), in_=w4_words[0].bitcast(I32))
+        load_w8(0)
+        load_x(1)
+        load_w4(0)
         load_scales(1, w4_scales)
-        for i in range(1, len(LOADS)):
+        load_w8(1)
+        load_w4(1)
+        for i in range(2, len(LOADS)):
             load_x(i)
 
         spread = []
@@ -194,6 +216,11 @@ def tile_mix_feat_tm_quad_silu_kernel(tc, x, w4_words, w4_scales, w8_words, w8_s
                 spread[h][:].rearrange("q (c p) -> q p c", c=PACK),
             )
 
+        def multiply_chunk(c):
+            for i in range(chunk_start[c] // P, (chunk_start[c] + CHUNKS[c]) // P):
+                for h in range(2):
+                    multiply(i, h)
+
         cast(0)
         square(0)
         cast(1)
@@ -202,48 +229,49 @@ def tile_mix_feat_tm_quad_silu_kernel(tc, x, w4_words, w4_scales, w8_words, w8_s
         quantize(1)
         nc.vector.tensor_copy(*bias_views(0))
         nc.scalar.copy(*bias_views(1))
+        for one_pass in (linear_pass, square_pass):
+            for i in range(2):
+                one_pass(i, 0)
         for i in range(2):
-            for h in range(2):
-                multiply(i, h)
-        add_bias(0, 0, BANK)
-        square(2)
+            multiply(i, 1)
         cast(2)
-        add_bias(0, BANK, M)
+        square(2)
+        for i in range(2):
+            add_bias(i, 0, BANK)
+            silu(i, 0, BANK)
         quantize(2)
         cast_gpsimd(3)
-        finish(0, 0, M)
         square(3)
-        add_bias(1, 0, BANK)
-        add_bias(1, BANK, M)
-        finish(1, 0, M)
+        for i in range(2):
+            add_bias(i, BANK, M)
+            silu(i, BANK, M)
+            store(i, 0, M)
 
         last = len(CHUNKS) - 1
-        for c in range(FIRST_SHARED, last):
+        for c in range(FIRST_SHARED, last - 1):
             i = chunk_start[c] // P
-            for step in range(2):
-                for h in range(2):
-                    multiply(i + step, h)
+            multiply_chunk(c)
             add_bias(i, 0, BANK)
             add_bias(i, BANK, M)
-            if c + 2 <= last:
-                square_vector(c + 2)
+            square_vector(c + 2)
             quantize(c + 1)
             finish(i, 0, M)
-            if c + 2 <= last:
-                cast_gpsimd(c + 2)
-                square(c + 2, VECTOR_SQUARES)
-            if c + 2 <= last:
+            cast_gpsimd(c + 2)
+            square(c + 2, VECTOR_SQUARES)
+            if c + 2 < last:
                 add_bias(i + 1, 0, BANK)
                 add_bias(i + 1, BANK, M)
                 finish(i + 1, 0, M)
             else:
                 finish_by_banks(i + 1)
 
-        i = chunk_start[last] // P
-        for step in range(2):
-            for h in range(2):
-                multiply(i + step, h)
+        i = chunk_start[last - 1] // P
+        multiply_chunk(last - 1)
         finish_by_banks(i)
+        quantize(last)
+        finish_by_banks(i + 1)
+        multiply_chunk(last)
+        finish_by_banks(i + 2)
         for lo, hi in [(0, BANK), (BANK, BANK + BANK // 2), (BANK + BANK // 2, M)]:
-            add_bias(i + 1, lo, hi)
-            finish(i + 1, lo, hi)
+            add_bias(i + 3, lo, hi)
+            finish(i + 3, lo, hi)

@@ -40,8 +40,6 @@ def tile_mix_feat_tm_quad_silu_kernel(tc, x, w4_words, w4_scales, w8_words, w8_s
         b_cols = keep.tile([P, 2, 8], F32, name="b_cols")
         ident = keep.tile([P, P], F32, name="ident")
         bias = keep.tile([P, M], F32, name="bias")
-        warm = keep.tile([P, 8], F32, name="warm")
-        warm_out = keep.tile([P, 8], F32, name="warm_out")
 
         load_start = [sum(LOADS[:i]) for i in range(len(LOADS))]
         raw = [keep.tile([P, PACK, w], F32, name="raw%d" % i) for i, w in enumerate(LOADS)]
@@ -188,10 +186,8 @@ def tile_mix_feat_tm_quad_silu_kernel(tc, x, w4_words, w4_scales, w8_words, w8_s
                 finish(i, lo, hi)
 
         nc.vector.memset(planes[:].rearrange("p f n -> p (f n)").bitcast(I32), 0)
-        nc.gpsimd.memset(warm[:], 0.0)
         nc.sync.dma_start(out=b_cols[:, :, 0:PACK], in_=b.rearrange("(h p c) -> p h c", h=2, c=PACK))
         load_x(0)
-        nc.scalar.activation(out=warm_out[:], in_=warm[:], func=ACT.Silu)
         make_identity(nc, ident[:])
         load_scales(0, w8_scales)
         load_w8(0)

@@ -20,17 +20,19 @@ P = 128
 PACK = 4
 BANK = 512
 RUN = 2
+LINEAR, SQUARE = 0, 1
 LOADS = [256, 256, 256, 256, 512]
-CHUNKS = [128, 128, 256, 256, 256, 256, 256]
+CHUNKS = [128, 128, 256, 256, 256, 256, 128, 128]
 FIRST_SHARED = 2
-VECTOR_SQUARES = 64
+WIDE = max(CHUNKS)
+VECTOR_SQUARES = {4: 64, 5: 64, 7: 64}
+GPSIMD_SQUARES = {}
 
 
 def tile_mix_feat_tm_quad_silu_kernel(tc, x, w4_words, w4_scales, w8_words, w8_scales, b, out):
     nc = tc.nc
     with ExitStack() as ctx:
         keep = ctx.enter_context(tc.tile_pool(name="keep", bufs=1))
-        pre_pool = ctx.enter_context(tc.tile_pool(name="pre", bufs=4))
         psum = ctx.enter_context(tc.psum_pool(name="psum", bufs=8))
         ctx.enter_context(tc.manual_schedule())
 
@@ -44,15 +46,15 @@ def tile_mix_feat_tm_quad_silu_kernel(tc, x, w4_words, w4_scales, w8_words, w8_s
         load_start = [sum(LOADS[:i]) for i in range(len(LOADS))]
         raw = [keep.tile([P, PACK, w], F32, name="raw%d" % i) for i, w in enumerate(LOADS)]
         chunk_start = [sum(CHUNKS[:c]) for c in range(len(CHUNKS))]
-        head_feats = [
-            keep.tile([P, 2, CHUNKS[c], PACK], BF16, name="feats%d" % c, align_bytes=64) for c in range(FIRST_SHARED)
-        ]
-        shared = keep.tile([P, 3, CHUNKS[FIRST_SHARED], PACK], BF16, name="shared", align_bytes=64)
+        last = len(CHUNKS) - 1
+        own_feats = {
+            c: keep.tile([P, 2, CHUNKS[c], PACK], BF16, name="feats%d" % c, align_bytes=64) for c in (0, 1, last)
+        }
+        shared = keep.tile([P, 3 * WIDE * PACK], BF16, name="shared", align_bytes=64)
         codes = [keep.tile([P, 2, w], U32, name="codes%d" % c, align_bytes=64) for c, w in enumerate(CHUNKS)]
         scales = [keep.tile([P, 2, w], U8, name="scales%d" % c, align_bytes=64) for c, w in enumerate(CHUNKS)]
         res = [keep.tile([P, M], F32, name="res%d" % i) for i in range(T // P)]
         acc = {}
-        pre = {}
 
         x_rows = x.rearrange("(p j) t -> p j t", j=PACK)
         w8_src = w8_words[0].rearrange("p n i -> p (n i)").bitcast(I32)
@@ -63,7 +65,7 @@ def tile_mix_feat_tm_quad_silu_kernel(tc, x, w4_words, w4_scales, w8_words, w8_s
             nc.sync.dma_start(out=raw[i][:], in_=x_rows[:, :, load_start[i] : load_start[i] + LOADS[i]])
 
         def load_scales(which, src):
-            for q in range(4):
+            for q in (0, 2, 1, 3):
                 nc.sync.dma_start(
                     out=planes[32 * q : 32 * q + 4, which, :].bitcast(I32),
                     in_=src[0, 4 * q : 4 * q + 4, :].bitcast(I32),
@@ -75,13 +77,17 @@ def tile_mix_feat_tm_quad_silu_kernel(tc, x, w4_words, w4_scales, w8_words, w8_s
         def load_w4(h):
             nc.sync.dma_start(out=w4[h][:].bitcast(I32), in_=w4_src[:, h * BANK // 2 : (h + 1) * BANK // 2])
 
-        def feats(c):
-            if c < FIRST_SHARED:
-                return head_feats[c][:]
-            return shared[:, c % 2 : c % 2 + 2, :, :]
+        def place(c, slot):
+            return slot if c in own_feats or c % 2 else 1 - slot
 
-        def linear_slot(c):
-            return 1 - c % 2
+        def feats(c):
+            if c in own_feats:
+                return own_feats[c][:]
+            lo = (WIDE - place(c, LINEAR) * CHUNKS[c]) * PACK
+            return shared[:, lo : lo + 2 * CHUNKS[c] * PACK].rearrange("p (f t j) -> p f t j", f=2, j=PACK)
+
+        def feature(c, slot):
+            return feats(c)[:, place(c, slot), :, :]
 
         def raw_rows(c):
             i = max(j for j in range(len(LOADS)) if load_start[j] <= chunk_start[c])
@@ -92,14 +98,14 @@ def tile_mix_feat_tm_quad_silu_kernel(tc, x, w4_words, w4_scales, w8_words, w8_s
             return raw_rows(c)[:, :, lo:hi].rearrange("p j (g i) -> p g j i", i=RUN)
 
         def feat_view(c, slot, lo, hi):
-            return feats(c)[:, slot, lo:hi, :].rearrange("p (g i) j -> p g j i", i=RUN)
+            return feature(c, slot)[:, lo:hi, :].rearrange("p (g i) j -> p g j i", i=RUN)
 
         def cast(c):
-            nc.vector.tensor_copy(out=feat_view(c, linear_slot(c), 0, CHUNKS[c]), in_=raw_view(c, 0, CHUNKS[c]))
+            nc.vector.tensor_copy(out=feat_view(c, LINEAR, 0, CHUNKS[c]), in_=raw_view(c, 0, CHUNKS[c]))
 
         def cast_gpsimd(c):
             nc.gpsimd.tensor_scalar(
-                out=feats(c)[:, linear_slot(c), :, :],
+                out=feature(c, LINEAR),
                 in0=raw_rows(c).rearrange("p j t -> p t j"),
                 scalar1=1.0,
                 scalar2=0.0,
@@ -107,15 +113,22 @@ def tile_mix_feat_tm_quad_silu_kernel(tc, x, w4_words, w4_scales, w8_words, w8_s
                 op1=ALU.add,
             )
 
-        def square(c, lo=0):
+        def square_gpsimd(c):
+            lo = VECTOR_SQUARES.get(c, 0)
+            hi = lo + GPSIMD_SQUARES[c]
+            src = raw_rows(c)[:, :, lo:hi].rearrange("p j t -> p t j")
+            nc.gpsimd.tensor_tensor(out=feature(c, SQUARE)[:, lo:hi, :], in0=src, in1=src, op=ALU.mult)
+
+        def square(c):
+            lo = VECTOR_SQUARES.get(c, 0) + GPSIMD_SQUARES.get(c, 0)
             nc.scalar.activation(
-                out=feat_view(c, 1 - linear_slot(c), lo, CHUNKS[c]), in_=raw_view(c, lo, CHUNKS[c]), func=ACT.Square
+                out=feat_view(c, SQUARE, lo, CHUNKS[c]), in_=raw_view(c, lo, CHUNKS[c]), func=ACT.Square
             )
 
         def square_vector(c):
-            src = raw_view(c, 0, VECTOR_SQUARES)
+            src = raw_view(c, 0, VECTOR_SQUARES[c])
             nc.vector.tensor_tensor(
-                out=feat_view(c, 1 - linear_slot(c), 0, VECTOR_SQUARES), in0=src, in1=src, op=ALU.mult
+                out=feat_view(c, SQUARE, 0, VECTOR_SQUARES[c]), in0=src, in1=src, op=ALU.mult
             )
 
         def quantize(c):
@@ -132,12 +145,11 @@ def tile_mix_feat_tm_quad_silu_kernel(tc, x, w4_words, w4_scales, w8_words, w8_s
         def linear_pass(i, h):
             c, cols = token_cols(i)
             n = slice(h * BANK, (h + 1) * BANK)
-            lin = linear_slot(c)
             acc[i, h] = psum.tile([P, BANK], F32, name="acc")
             nc.tensor.matmul_mx(
                 out=acc[i, h][:],
-                lhsT=codes[c][:, lin, cols].bitcast(FP8X4),
-                lhsT_scale=scales[c][:, lin, cols],
+                lhsT=codes[c][:, place(c, LINEAR), cols].bitcast(FP8X4),
+                lhsT_scale=scales[c][:, place(c, LINEAR), cols],
                 rhs=w8[h][:].bitcast(FP8X4),
                 rhs_scale=planes[:, 0, n],
                 start=True,
@@ -147,11 +159,10 @@ def tile_mix_feat_tm_quad_silu_kernel(tc, x, w4_words, w4_scales, w8_words, w8_s
         def square_pass(i, h):
             c, cols = token_cols(i)
             n = slice(h * BANK, (h + 1) * BANK)
-            lin = linear_slot(c)
             nc.tensor.matmul_mx(
                 out=acc[i, h][:],
-                lhsT=codes[c][:, 1 - lin, cols].bitcast(FP8X4),
-                lhsT_scale=scales[c][:, 1 - lin, cols],
+                lhsT=codes[c][:, place(c, SQUARE), cols].bitcast(FP8X4),
+                lhsT_scale=scales[c][:, place(c, SQUARE), cols],
                 rhs=w4[h][:].bitcast(FP4X4),
                 rhs_scale=planes[:, 1, n],
                 start=False,
@@ -163,15 +174,13 @@ def tile_mix_feat_tm_quad_silu_kernel(tc, x, w4_words, w4_scales, w8_words, w8_s
             square_pass(i, h)
 
         def add_bias(i, lo, hi):
-            if i not in pre:
-                pre[i] = pre_pool.tile([P, M], F32, name="pre")
             h = lo // BANK
             nc.vector.tensor_tensor(
-                out=pre[i][:, lo:hi], in0=acc[i, h][:, lo - h * BANK : hi - h * BANK], in1=bias[:, lo:hi], op=ALU.add
+                out=res[i][:, lo:hi], in0=acc[i, h][:, lo - h * BANK : hi - h * BANK], in1=bias[:, lo:hi], op=ALU.add
             )
 
         def silu(i, lo, hi):
-            nc.scalar.activation(out=res[i][:, lo:hi], in_=pre[i][:, lo:hi], func=ACT.Silu)
+            nc.scalar.activation(out=res[i][:, lo:hi], in_=res[i][:, lo:hi], func=ACT.Silu)
 
         def store(i, lo, hi):
             nc.sync.dma_start(out=out[i * P : (i + 1) * P, lo:hi], in_=res[i][:, lo:hi])
@@ -180,30 +189,32 @@ def tile_mix_feat_tm_quad_silu_kernel(tc, x, w4_words, w4_scales, w8_words, w8_s
             silu(i, lo, hi)
             store(i, lo, hi)
 
-        def finish_by_banks(i):
-            for lo, hi in [(0, BANK), (BANK, M)]:
-                add_bias(i, lo, hi)
-                finish(i, lo, hi)
+        def empty(i, h):
+            add_bias(i, h * BANK, (h + 1) * BANK)
 
         nc.vector.memset(planes[:].rearrange("p f n -> p (f n)").bitcast(I32), 0)
-        nc.sync.dma_start(out=b_cols[:, :, 0:PACK], in_=b.rearrange("(h p c) -> p h c", h=2, c=PACK))
         load_x(0)
+        nc.sync.dma_start(out=b_cols[:, :, 0:PACK], in_=b.rearrange("(h p c) -> p h c", h=2, c=PACK))
         make_identity(nc, ident[:])
+        warm = keep.tile([P, 8], F32, name="warm")
+        nc.scalar.activation(out=warm[:, 0:1], in_=ident[:, 0:1], func=ACT.Silu)
         load_scales(0, w8_scales)
         load_w8(0)
-        load_x(1)
         load_w4(0)
         load_scales(1, w4_scales)
+        load_x(1)
         load_w8(1)
         load_w4(1)
-        for i in range(2, len(LOADS)):
-            load_x(i)
+        load_x(2)
+        load_x(3)
+        load_x(4)
 
         spread = []
         for h in range(2):
             bank = psum.tile([P, BANK], F32, name="acc")
             for c in range(PACK):
-                nc.tensor.transpose(bank[:, c * P : (c + 1) * P], b_cols[:, h, c : c + 1].to_broadcast([P, P]), ident[:])
+                col = b_cols[:, h, c : c + 1]
+                nc.tensor.transpose(bank[:, c * P : (c + 1) * P], col.to_broadcast([P, P]), ident[:])
             spread.append(bank)
 
         def bias_views(h):
@@ -217,6 +228,13 @@ def tile_mix_feat_tm_quad_silu_kernel(tc, x, w4_words, w4_scales, w8_words, w8_s
                 for h in range(2):
                     multiply(i, h)
 
+        def finish_tile(i):
+            if i < 7:
+                finish(i, 0, M)
+            else:
+                finish(i, 0, BANK)
+                finish(i, BANK, M)
+
         cast(0)
         square(0)
         cast(1)
@@ -225,49 +243,60 @@ def tile_mix_feat_tm_quad_silu_kernel(tc, x, w4_words, w4_scales, w8_words, w8_s
         quantize(1)
         nc.vector.tensor_copy(*bias_views(0))
         nc.scalar.copy(*bias_views(1))
-        for one_pass in (linear_pass, square_pass):
+        for h in range(2):
             for i in range(2):
-                one_pass(i, 0)
-        for i in range(2):
-            multiply(i, 1)
-        cast(2)
+                multiply(i, h)
+        empty(0, 0)
         square(2)
-        for i in range(2):
-            add_bias(i, 0, BANK)
-            silu(i, 0, BANK)
+        silu(0, 0, BANK)
+        cast(2)
+        empty(1, 0)
+        silu(1, 0, BANK)
         quantize(2)
         cast_gpsimd(3)
+        multiply_chunk(2)
         square(3)
         for i in range(2):
-            add_bias(i, BANK, M)
+            empty(i, 1)
             silu(i, BANK, M)
             store(i, 0, M)
 
-        last = len(CHUNKS) - 1
-        for c in range(FIRST_SHARED, last - 1):
+        for c in (2, 3, 4):
             i = chunk_start[c] // P
-            multiply_chunk(c)
-            add_bias(i, 0, BANK)
-            add_bias(i, BANK, M)
-            square_vector(c + 2)
+            empty(i, 0)
+            empty(i, 1)
+            if c + 2 in VECTOR_SQUARES:
+                square_vector(c + 2)
             quantize(c + 1)
-            finish(i, 0, M)
             cast_gpsimd(c + 2)
-            square(c + 2, VECTOR_SQUARES)
-            if c + 2 < last:
-                add_bias(i + 1, 0, BANK)
-                add_bias(i + 1, BANK, M)
-                finish(i + 1, 0, M)
-            else:
-                finish_by_banks(i + 1)
-
-        i = chunk_start[last - 1] // P
-        multiply_chunk(last - 1)
-        finish_by_banks(i)
+            if c + 3 == last:
+                cast_gpsimd(last)
+            finish_tile(i)
+            square(c + 2)
+            multiply(i + 2, 0)
+            multiply(i + 2, 1)
+            empty(i + 1, 0)
+            empty(i + 1, 1)
+            finish_tile(i + 1)
+            multiply(i + 3, 0)
+            multiply(i + 3, 1)
+        empty(8, 0)
+        empty(8, 1)
+        if last in VECTOR_SQUARES:
+            square_vector(last)
+        quantize(6)
+        if VECTOR_SQUARES.get(last, 0) < CHUNKS[last]:
+            square(last)
+        finish_tile(8)
+        multiply_chunk(6)
+        empty(9, 0)
+        empty(9, 1)
         quantize(last)
-        finish_by_banks(i + 1)
+        finish_tile(9)
         multiply_chunk(last)
-        finish_by_banks(i + 2)
+        empty(10, 0)
+        empty(10, 1)
+        finish_tile(10)
         for lo, hi in [(0, BANK), (BANK, BANK + BANK // 2), (BANK + BANK // 2, M)]:
-            add_bias(i + 3, lo, hi)
-            finish(i + 3, lo, hi)
+            add_bias(11, lo, hi)
+            finish(11, lo, hi)

@@ -25,8 +25,8 @@ LOADS = [256, 256, 256, 256, 512]
 CHUNKS = [128, 128, 256, 256, 256, 256, 128, 128]
 FIRST_SHARED = 2
 WIDE = max(CHUNKS)
-VECTOR_SQUARES = {4: 64, 5: 64, 7: 64}
-GPSIMD_SQUARES = {}
+VECTOR_SQUARES = {2: 64, 4: 32, 5: 64, 7: 64}
+GPSIMD_SQUARES = {3: 64}
 
 
 def tile_mix_feat_tm_quad_silu_kernel(tc, x, w4_words, w4_scales, w8_words, w8_scales, b, out):
@@ -65,7 +65,7 @@ def tile_mix_feat_tm_quad_silu_kernel(tc, x, w4_words, w4_scales, w8_words, w8_s
             nc.sync.dma_start(out=raw[i][:], in_=x_rows[:, :, load_start[i] : load_start[i] + LOADS[i]])
 
         def load_scales(which, src):
-            for q in (0, 2, 1, 3):
+            for q in range(4):
                 nc.sync.dma_start(
                     out=planes[32 * q : 32 * q + 4, which, :].bitcast(I32),
                     in_=src[0, 4 * q : 4 * q + 4, :].bitcast(I32),
@@ -193,19 +193,19 @@ def tile_mix_feat_tm_quad_silu_kernel(tc, x, w4_words, w4_scales, w8_words, w8_s
             add_bias(i, h * BANK, (h + 1) * BANK)
 
         nc.vector.memset(planes[:].rearrange("p f n -> p (f n)").bitcast(I32), 0)
-        load_x(0)
         nc.sync.dma_start(out=b_cols[:, :, 0:PACK], in_=b.rearrange("(h p c) -> p h c", h=2, c=PACK))
+        load_x(0)
         make_identity(nc, ident[:])
         warm = keep.tile([P, 8], F32, name="warm")
         nc.scalar.activation(out=warm[:, 0:1], in_=ident[:, 0:1], func=ACT.Silu)
         load_scales(0, w8_scales)
         load_w8(0)
+        load_x(1)
         load_w4(0)
         load_scales(1, w4_scales)
-        load_x(1)
+        load_x(2)
         load_w8(1)
         load_w4(1)
-        load_x(2)
         load_x(3)
         load_x(4)
 
@@ -243,25 +243,44 @@ def tile_mix_feat_tm_quad_silu_kernel(tc, x, w4_words, w4_scales, w8_words, w8_s
         quantize(1)
         nc.vector.tensor_copy(*bias_views(0))
         nc.scalar.copy(*bias_views(1))
-        for h in range(2):
+        for one_pass in (linear_pass, square_pass):
             for i in range(2):
-                multiply(i, h)
-        empty(0, 0)
-        square(2)
-        silu(0, 0, BANK)
+                one_pass(i, 0)
+        square_vector(2)
         cast(2)
-        empty(1, 0)
-        silu(1, 0, BANK)
+        square(2)
         quantize(2)
         cast_gpsimd(3)
-        multiply_chunk(2)
+        square_gpsimd(3)
+        for i in (2, 3):
+            multiply(i, 0)
+        for i in range(4):
+            multiply(i, 1)
         square(3)
+        for i in range(4):
+            empty(i, 0)
+            if i < 3:
+                silu(i, 0, BANK)
         for i in range(2):
             empty(i, 1)
             silu(i, BANK, M)
             store(i, 0, M)
+        if 4 in VECTOR_SQUARES:
+            square_vector(4)
+        quantize(3)
+        cast_gpsimd(4)
+        multiply(4, 0)
+        multiply(4, 1)
+        square(4)
+        empty(2, 1)
+        silu(2, BANK, M)
+        store(2, 0, M)
+        empty(3, 1)
+        finish(3, 0, M)
+        multiply(5, 0)
+        multiply(5, 1)
 
-        for c in (2, 3, 4):
+        for c in (3, 4):
             i = chunk_start[c] // P
             empty(i, 0)
             empty(i, 1)

@@ -19,13 +19,13 @@ ALU = mybir.AluOpType
 P = 128
 PACK = 4
 BANK = 512
-RUN = 2
+RUN = 4
 LINEAR, SQUARE = 0, 1
 LOADS = [256, 256, 256, 256, 512]
 CHUNKS = [128, 128, 256, 256, 256, 256, 128, 128]
 FIRST_SHARED = 2
 WIDE = max(CHUNKS)
-VECTOR_SQUARES = {2: 64, 4: 32, 5: 64, 7: 64}
+VECTOR_SQUARES = {2: 64, 5: 64, 7: 64}
 GPSIMD_SQUARES = {3: 64}
 
 
@@ -260,11 +260,10 @@ def tile_mix_feat_tm_quad_silu_kernel(tc, x, w4_words, w4_scales, w8_words, w8_s
         for i in range(4):
             empty(i, 0)
             if i < 3:
-                silu(i, 0, BANK)
+                finish(i, 0, BANK)
         for i in range(2):
             empty(i, 1)
-            silu(i, BANK, M)
-            store(i, 0, M)
+            finish(i, BANK, M)
         if 4 in VECTOR_SQUARES:
             square_vector(4)
         quantize(3)
@@ -273,8 +272,7 @@ def tile_mix_feat_tm_quad_silu_kernel(tc, x, w4_words, w4_scales, w8_words, w8_s
         multiply(4, 1)
         square(4)
         empty(2, 1)
-        silu(2, BANK, M)
-        store(2, 0, M)
+        finish(2, BANK, M)
         empty(3, 1)
         finish(3, 0, M)
         multiply(5, 0)
@@ -316,6 +314,6 @@ def tile_mix_feat_tm_quad_silu_kernel(tc, x, w4_words, w4_scales, w8_words, w8_s
         empty(10, 0)
         empty(10, 1)
         finish_tile(10)
-        for lo, hi in [(0, BANK), (BANK, BANK + BANK // 2), (BANK + BANK // 2, M)]:
+        for lo, hi in [(0, BANK), (BANK, M)]:
             add_bias(11, lo, hi)
             finish(11, lo, hi)

@@ -196,8 +196,6 @@ def tile_mix_feat_tm_quad_silu_kernel(tc, x, w4_words, w4_scales, w8_words, w8_s
         nc.sync.dma_start(out=b_cols[:, :, 0:PACK], in_=b.rearrange("(h p c) -> p h c", h=2, c=PACK))
         load_x(0)
         make_identity(nc, ident[:])
-        warm = keep.tile([P, 8], F32, name="warm")
-        nc.scalar.activation(out=warm[:, 0:1], in_=ident[:, 0:1], func=ACT.Silu)
         load_scales(0, w8_scales)
         load_w8(0)
         load_x(1)
@@ -256,11 +254,12 @@ def tile_mix_feat_tm_quad_silu_kernel(tc, x, w4_words, w4_scales, w8_words, w8_s
             multiply(i, 0)
         for i in range(4):
             multiply(i, 1)
-        square(3)
         for i in range(4):
             empty(i, 0)
             if i < 3:
                 finish(i, 0, BANK)
+            if i == 0:
+                square(3)
         for i in range(2):
             empty(i, 1)
             finish(i, BANK, M)

@@ -25,8 +25,8 @@ LOADS = [256, 256, 256, 256, 512]
 CHUNKS = [128, 128, 256, 256, 256, 256, 128, 128]
 FIRST_SHARED = 2
 WIDE = max(CHUNKS)
-VECTOR_SQUARES = {2: 64, 5: 64, 7: 64}
-GPSIMD_SQUARES = {3: 64}
+VECTOR_SQUARES = {2: 64, 4: 32, 5: 64, 7: 64}
+GPSIMD_SQUARES = {3: 96}
 
 
 def tile_mix_feat_tm_quad_silu_kernel(tc, x, w4_words, w4_scales, w8_words, w8_scales, b, out):
@@ -138,6 +138,14 @@ def tile_mix_feat_tm_quad_silu_kernel(tc, x, w4_words, w4_scales, w8_words, w8_s
                 in_=feats(c).rearrange("p f t j -> p (f t j)"),
             )
 
+        def quantize_feature(c, slot):
+            f = place(c, slot)
+            nc.vector.quantize_mx(
+                out=codes[c][:, f, :].bitcast(FP8X4),
+                scales=scales[c][:, f, :],
+                in_=feature(c, slot).rearrange("p t j -> p (t j)"),
+            )
+
         def token_cols(i):
             c = max(j for j in range(len(CHUNKS)) if chunk_start[j] <= i * P)
             return c, slice(i * P - chunk_start[c], i * P - chunk_start[c] + P)
@@ -244,10 +252,11 @@ def tile_mix_feat_tm_quad_silu_kernel(tc, x, w4_words, w4_scales, w8_words, w8_s
         for one_pass in (linear_pass, square_pass):
             for i in range(2):
                 one_pass(i, 0)
-        square_vector(2)
         cast(2)
+        square_vector(2)
         square(2)
-        quantize(2)
+        quantize_feature(2, LINEAR)
+        quantize_feature(2, SQUARE)
         cast_gpsimd(3)
         square_gpsimd(3)
         for i in (2, 3):

@@ -19,55 +19,58 @@ ALU = mybir.AluOpType
 P = 128
 PACK = 4
 BANK = 512
+PSUM_BANKS = 8
+TILES = T // P
 RUN = 4
 LINEAR, SQUARE = 0, 1
+
 LOADS = [256, 256, 256, 256, 512]
 CHUNKS = [128, 128, 256, 256, 256, 256, 128, 128]
-FIRST_SHARED = 2
 WIDE = max(CHUNKS)
-VECTOR_SQUARES = {2: 64, 4: 32, 5: 64, 7: 64}
-GPSIMD_SQUARES = {3: 96}
+LAST = len(CHUNKS) - 1
+OWN_BUFFER = (0, 1)
+VECTOR_SQUARES = {2: 64, 4: 64, 5: 48}
+GPSIMD_SQUARES = {3: 96, 5: 48, 6: 48, 7: 48}
+BY_BANKS_FROM = 7
 
 
 def tile_mix_feat_tm_quad_silu_kernel(tc, x, w4_words, w4_scales, w8_words, w8_scales, b, out):
     nc = tc.nc
     with ExitStack() as ctx:
         keep = ctx.enter_context(tc.tile_pool(name="keep", bufs=1))
-        psum = ctx.enter_context(tc.psum_pool(name="psum", bufs=8))
+        psum = ctx.enter_context(tc.psum_pool(name="psum", bufs=PSUM_BANKS))
         ctx.enter_context(tc.manual_schedule())
 
         w8 = [keep.tile([P, BANK], U32, name="w8_%d" % h, align_bytes=64) for h in range(2)]
         w4 = [keep.tile([P, 2 * BANK], U8, name="w4_%d" % h, align_bytes=64) for h in range(2)]
         planes = keep.tile([P, 2, M], U8, name="planes", align_bytes=64)
-        b_cols = keep.tile([P, 2, 8], F32, name="b_cols")
+        b_cols = keep.tile([P, 2, 2 * PACK], F32, name="b_cols")
         ident = keep.tile([P, P], F32, name="ident")
         bias = keep.tile([P, M], F32, name="bias")
 
         load_start = [sum(LOADS[:i]) for i in range(len(LOADS))]
         raw = [keep.tile([P, PACK, w], F32, name="raw%d" % i) for i, w in enumerate(LOADS)]
         chunk_start = [sum(CHUNKS[:c]) for c in range(len(CHUNKS))]
-        last = len(CHUNKS) - 1
         own_feats = {
-            c: keep.tile([P, 2, CHUNKS[c], PACK], BF16, name="feats%d" % c, align_bytes=64) for c in (0, 1, last)
+            c: keep.tile([P, 2, CHUNKS[c], PACK], BF16, name="feats%d" % c, align_bytes=64) for c in OWN_BUFFER
         }
         shared = keep.tile([P, 3 * WIDE * PACK], BF16, name="shared", align_bytes=64)
         codes = [keep.tile([P, 2, w], U32, name="codes%d" % c, align_bytes=64) for c, w in enumerate(CHUNKS)]
         scales = [keep.tile([P, 2, w], U8, name="scales%d" % c, align_bytes=64) for c, w in enumerate(CHUNKS)]
-        res = [keep.tile([P, M], F32, name="res%d" % i) for i in range(T // P)]
+        res = [keep.tile([P, M], F32, name="res%d" % i) for i in range(TILES)]
         acc = {}
 
         x_rows = x.rearrange("(p j) t -> p j t", j=PACK)
         w8_src = w8_words[0].rearrange("p n i -> p (n i)").bitcast(I32)
-
         w4_src = w4_words[0].bitcast(I32)
 
         def load_x(i):
             nc.sync.dma_start(out=raw[i][:], in_=x_rows[:, :, load_start[i] : load_start[i] + LOADS[i]])
 
-        def load_scales(which, src):
+        def load_scales(feat, src):
             for q in range(4):
                 nc.sync.dma_start(
-                    out=planes[32 * q : 32 * q + 4, which, :].bitcast(I32),
+                    out=planes[32 * q : 32 * q + 4, feat, :].bitcast(I32),
                     in_=src[0, 4 * q : 4 * q + 4, :].bitcast(I32),
                 )
 
@@ -77,138 +80,128 @@ def tile_mix_feat_tm_quad_silu_kernel(tc, x, w4_words, w4_scales, w8_words, w8_s
         def load_w4(h):
             nc.sync.dma_start(out=w4[h][:].bitcast(I32), in_=w4_src[:, h * BANK // 2 : (h + 1) * BANK // 2])
 
-        def place(c, slot):
-            return slot if c in own_feats or c % 2 else 1 - slot
+        def place(c, feat):
+            return feat if c in OWN_BUFFER or c % 2 else 1 - feat
 
         def feats(c):
-            if c in own_feats:
+            if c in OWN_BUFFER:
                 return own_feats[c][:]
-            lo = (WIDE - place(c, LINEAR) * CHUNKS[c]) * PACK
+            xb_start = WIDE + (CHUNKS[c] if c == LAST else 0)
+            lo = (xb_start - place(c, LINEAR) * CHUNKS[c]) * PACK
             return shared[:, lo : lo + 2 * CHUNKS[c] * PACK].rearrange("p (f t j) -> p f t j", f=2, j=PACK)
 
-        def feature(c, slot):
-            return feats(c)[:, place(c, slot), :, :]
+        def feature(c, feat):
+            return feats(c)[:, place(c, feat), :, :]
 
-        def raw_rows(c):
+        def raw_tokens(c, lo, hi):
             i = max(j for j in range(len(LOADS)) if load_start[j] <= chunk_start[c])
             t0 = chunk_start[c] - load_start[i]
-            return raw[i][:, :, t0 : t0 + CHUNKS[c]]
+            return raw[i][:, :, t0 + lo : t0 + hi]
 
-        def raw_view(c, lo, hi):
-            return raw_rows(c)[:, :, lo:hi].rearrange("p j (g i) -> p g j i", i=RUN)
+        def raw_runs(c, lo, hi):
+            return raw_tokens(c, lo, hi).rearrange("p j (g i) -> p g j i", i=RUN)
 
-        def feat_view(c, slot, lo, hi):
-            return feature(c, slot)[:, lo:hi, :].rearrange("p (g i) j -> p g j i", i=RUN)
+        def feature_runs(c, feat, lo, hi):
+            return feature(c, feat)[:, lo:hi, :].rearrange("p (g i) j -> p g j i", i=RUN)
 
-        def cast(c):
-            nc.vector.tensor_copy(out=feat_view(c, LINEAR, 0, CHUNKS[c]), in_=raw_view(c, 0, CHUNKS[c]))
+        def cast_vector(c):
+            nc.vector.tensor_copy(out=feature_runs(c, LINEAR, 0, CHUNKS[c]), in_=raw_runs(c, 0, CHUNKS[c]))
 
         def cast_gpsimd(c):
             nc.gpsimd.tensor_scalar(
-                out=feature(c, LINEAR),
-                in0=raw_rows(c).rearrange("p j t -> p t j"),
+                out=shared[:, WIDE * PACK : 2 * WIDE * PACK].rearrange("p (t j) -> p t j", j=PACK),
+                in0=raw_tokens(c, 0, WIDE).rearrange("p j t -> p t j"),
                 scalar1=1.0,
                 scalar2=0.0,
                 op0=ALU.mult,
                 op1=ALU.add,
             )
 
+        def square_vector(c):
+            src = raw_runs(c, 0, VECTOR_SQUARES[c])
+            nc.vector.tensor_tensor(out=feature_runs(c, SQUARE, 0, VECTOR_SQUARES[c]), in0=src, in1=src, op=ALU.mult)
+
         def square_gpsimd(c):
             lo = VECTOR_SQUARES.get(c, 0)
             hi = lo + GPSIMD_SQUARES[c]
-            src = raw_rows(c)[:, :, lo:hi].rearrange("p j t -> p t j")
+            src = raw_tokens(c, lo, hi).rearrange("p j t -> p t j")
             nc.gpsimd.tensor_tensor(out=feature(c, SQUARE)[:, lo:hi, :], in0=src, in1=src, op=ALU.mult)
 
-        def square(c):
+        def square_scalar(c):
             lo = VECTOR_SQUARES.get(c, 0) + GPSIMD_SQUARES.get(c, 0)
             nc.scalar.activation(
-                out=feat_view(c, SQUARE, lo, CHUNKS[c]), in_=raw_view(c, lo, CHUNKS[c]), func=ACT.Square
+                out=feature_runs(c, SQUARE, lo, CHUNKS[c]), in_=raw_runs(c, lo, CHUNKS[c]), func=ACT.Square
             )
 
-        def square_vector(c):
-            src = raw_view(c, 0, VECTOR_SQUARES[c])
-            nc.vector.tensor_tensor(
-                out=feat_view(c, SQUARE, 0, VECTOR_SQUARES[c]), in0=src, in1=src, op=ALU.mult
-            )
-
-        def quantize(c):
+        def quantize_both(c):
             nc.vector.quantize_mx(
                 out=codes[c][:].rearrange("p f t -> p (f t)").bitcast(FP8X4),
                 scales=scales[c][:].rearrange("p f t -> p (f t)"),
                 in_=feats(c).rearrange("p f t j -> p (f t j)"),
             )
 
-        def quantize_feature(c, slot):
-            f = place(c, slot)
-            nc.vector.quantize_mx(
-                out=codes[c][:, f, :].bitcast(FP8X4),
-                scales=scales[c][:, f, :],
-                in_=feature(c, slot).rearrange("p t j -> p (t j)"),
-            )
+        def quantize_in_turn(c):
+            for feat in (LINEAR, SQUARE):
+                nc.vector.quantize_mx(
+                    out=codes[c][:, place(c, feat), :].bitcast(FP8X4),
+                    scales=scales[c][:, place(c, feat), :],
+                    in_=feature(c, feat).rearrange("p t j -> p (t j)"),
+                )
 
-        def token_cols(i):
+        def one_pass(i, h, feat):
             c = max(j for j in range(len(CHUNKS)) if chunk_start[j] <= i * P)
-            return c, slice(i * P - chunk_start[c], i * P - chunk_start[c] + P)
-
-        def linear_pass(i, h):
-            c, cols = token_cols(i)
-            n = slice(h * BANK, (h + 1) * BANK)
-            acc[i, h] = psum.tile([P, BANK], F32, name="acc")
+            cols = slice(i * P - chunk_start[c], (i + 1) * P - chunk_start[c])
+            if feat == LINEAR:
+                acc[i, h] = psum.tile([P, BANK], F32, name="acc")
             nc.tensor.matmul_mx(
                 out=acc[i, h][:],
-                lhsT=codes[c][:, place(c, LINEAR), cols].bitcast(FP8X4),
-                lhsT_scale=scales[c][:, place(c, LINEAR), cols],
-                rhs=w8[h][:].bitcast(FP8X4),
-                rhs_scale=planes[:, 0, n],
-                start=True,
-                stop=False,
-            )
-
-        def square_pass(i, h):
-            c, cols = token_cols(i)
-            n = slice(h * BANK, (h + 1) * BANK)
-            nc.tensor.matmul_mx(
-                out=acc[i, h][:],
-                lhsT=codes[c][:, place(c, SQUARE), cols].bitcast(FP8X4),
-                lhsT_scale=scales[c][:, place(c, SQUARE), cols],
-                rhs=w4[h][:].bitcast(FP4X4),
-                rhs_scale=planes[:, 1, n],
-                start=False,
-                stop=True,
+                lhsT=codes[c][:, place(c, feat), cols].bitcast(FP8X4),
+                lhsT_scale=scales[c][:, place(c, feat), cols],
+                rhs=w8[h][:].bitcast(FP8X4) if feat == LINEAR else w4[h][:].bitcast(FP4X4),
+                rhs_scale=planes[:, feat, h * BANK : (h + 1) * BANK],
+                start=feat == LINEAR,
+                stop=feat == SQUARE,
             )
 
         def multiply(i, h):
-            linear_pass(i, h)
-            square_pass(i, h)
+            one_pass(i, h, LINEAR)
+            one_pass(i, h, SQUARE)
 
-        def add_bias(i, lo, hi):
-            h = lo // BANK
-            nc.vector.tensor_tensor(
-                out=res[i][:, lo:hi], in0=acc[i, h][:, lo - h * BANK : hi - h * BANK], in1=bias[:, lo:hi], op=ALU.add
-            )
-
-        def silu(i, lo, hi):
-            nc.scalar.activation(out=res[i][:, lo:hi], in_=res[i][:, lo:hi], func=ACT.Silu)
-
-        def store(i, lo, hi):
-            nc.sync.dma_start(out=out[i * P : (i + 1) * P, lo:hi], in_=res[i][:, lo:hi])
-
-        def finish(i, lo, hi):
-            silu(i, lo, hi)
-            store(i, lo, hi)
+        def multiply_tile(i):
+            multiply(i, 0)
+            multiply(i, 1)
 
         def empty(i, h):
-            add_bias(i, h * BANK, (h + 1) * BANK)
+            n = slice(h * BANK, (h + 1) * BANK)
+            nc.vector.tensor_tensor(out=res[i][:, n], in0=acc[i, h][:], in1=bias[:, n], op=ALU.add)
+
+        def empty_tile(i):
+            empty(i, 0)
+            empty(i, 1)
+
+        def finish(i, lo, hi):
+            nc.scalar.activation(out=res[i][:, lo:hi], in_=res[i][:, lo:hi], func=ACT.Silu)
+            nc.sync.dma_start(out=out[i * P : (i + 1) * P, lo:hi], in_=res[i][:, lo:hi])
+
+        def finish_bank(i, h):
+            finish(i, h * BANK, (h + 1) * BANK)
+
+        def finish_tile(i):
+            if i < BY_BANKS_FROM:
+                finish(i, 0, M)
+            else:
+                finish_bank(i, 0)
+                finish_bank(i, 1)
 
         nc.vector.memset(planes[:].rearrange("p f n -> p (f n)").bitcast(I32), 0)
         nc.sync.dma_start(out=b_cols[:, :, 0:PACK], in_=b.rearrange("(h p c) -> p h c", h=2, c=PACK))
         load_x(0)
         make_identity(nc, ident[:])
-        load_scales(0, w8_scales)
+        load_scales(LINEAR, w8_scales)
         load_w8(0)
         load_x(1)
         load_w4(0)
-        load_scales(1, w4_scales)
+        load_scales(SQUARE, w4_scales)
         load_x(2)
         load_w8(1)
         load_w4(1)
@@ -229,99 +222,72 @@ def tile_mix_feat_tm_quad_silu_kernel(tc, x, w4_words, w4_scales, w8_words, w8_s
                 spread[h][:].rearrange("q (c p) -> q p c", c=PACK),
             )
 
-        def multiply_chunk(c):
-            for i in range(chunk_start[c] // P, (chunk_start[c] + CHUNKS[c]) // P):
-                for h in range(2):
-                    multiply(i, h)
-
-        def finish_tile(i):
-            if i < 7:
-                finish(i, 0, M)
-            else:
-                finish(i, 0, BANK)
-                finish(i, BANK, M)
-
-        cast(0)
-        square(0)
-        cast(1)
-        square(1)
-        quantize(0)
-        quantize(1)
+        for c in OWN_BUFFER:
+            cast_vector(c)
+            square_scalar(c)
+        for c in OWN_BUFFER:
+            quantize_both(c)
         nc.vector.tensor_copy(*bias_views(0))
         nc.scalar.copy(*bias_views(1))
-        for one_pass in (linear_pass, square_pass):
-            for i in range(2):
-                one_pass(i, 0)
-        cast(2)
+        for feat in (LINEAR, SQUARE):
+            for i in (0, 1):
+                one_pass(i, 0, feat)
+        cast_vector(2)
         square_vector(2)
-        square(2)
-        quantize_feature(2, LINEAR)
-        quantize_feature(2, SQUARE)
+        square_scalar(2)
+        quantize_in_turn(2)
         cast_gpsimd(3)
         square_gpsimd(3)
+
         for i in (2, 3):
             multiply(i, 0)
         for i in range(4):
             multiply(i, 1)
-        for i in range(4):
+        empty(0, 0)
+        finish_bank(0, 0)
+        square_scalar(3)
+        for i in (1, 2):
             empty(i, 0)
-            if i < 3:
-                finish(i, 0, BANK)
-            if i == 0:
-                square(3)
-        for i in range(2):
+            finish_bank(i, 0)
+        empty(3, 0)
+        for i in (0, 1):
             empty(i, 1)
-            finish(i, BANK, M)
-        if 4 in VECTOR_SQUARES:
-            square_vector(4)
-        quantize(3)
+            finish_bank(i, 1)
+        square_vector(4)
+        quantize_in_turn(3)
         cast_gpsimd(4)
-        multiply(4, 0)
-        multiply(4, 1)
-        square(4)
+        square_gpsimd(5)
+        multiply_tile(4)
+        square_scalar(4)
         empty(2, 1)
-        finish(2, BANK, M)
+        finish_bank(2, 1)
         empty(3, 1)
-        finish(3, 0, M)
-        multiply(5, 0)
-        multiply(5, 1)
+        finish_tile(3)
+        multiply_tile(5)
 
         for c in (3, 4):
             i = chunk_start[c] // P
-            empty(i, 0)
-            empty(i, 1)
+            empty_tile(i)
             if c + 2 in VECTOR_SQUARES:
                 square_vector(c + 2)
-            quantize(c + 1)
+            quantize_in_turn(c + 1)
             cast_gpsimd(c + 2)
-            if c + 3 == last:
-                cast_gpsimd(last)
+            square_gpsimd(c + 3)
             finish_tile(i)
-            square(c + 2)
-            multiply(i + 2, 0)
-            multiply(i + 2, 1)
-            empty(i + 1, 0)
-            empty(i + 1, 1)
+            square_scalar(c + 2)
+            multiply_tile(i + 2)
+            empty_tile(i + 1)
             finish_tile(i + 1)
-            multiply(i + 3, 0)
-            multiply(i + 3, 1)
-        empty(8, 0)
-        empty(8, 1)
-        if last in VECTOR_SQUARES:
-            square_vector(last)
-        quantize(6)
-        if VECTOR_SQUARES.get(last, 0) < CHUNKS[last]:
-            square(last)
-        finish_tile(8)
-        multiply_chunk(6)
-        empty(9, 0)
-        empty(9, 1)
-        quantize(last)
-        finish_tile(9)
-        multiply_chunk(last)
-        empty(10, 0)
-        empty(10, 1)
-        finish_tile(10)
-        for lo, hi in [(0, BANK), (BANK, M)]:
-            add_bias(11, lo, hi)
-            finish(11, lo, hi)
+            multiply_tile(i + 3)
+
+        for c in (LAST - 1, LAST):
+            i = chunk_start[c] // P
+            empty_tile(i - 2)
+            quantize_both(c)
+            if c < LAST:
+                square_scalar(LAST)
+            finish_tile(i - 2)
+            multiply_tile(i)
+        for i in (TILES - 2, TILES - 1):
+            empty_tile(i)
+            finish_tile(i)

@@ -29,7 +29,7 @@ CHUNKS = [128, 128, 256, 256, 256, 256, 128, 128]
 WIDE = max(CHUNKS)
 LAST = len(CHUNKS) - 1
 OWN_BUFFER = (0, 1)
-VECTOR_SQUARES = {2: 64, 4: 64, 5: 48}
+VECTOR_SQUARES = {2: 64, 4: 32, 5: 48}
 GPSIMD_SQUARES = {3: 96, 5: 48, 6: 48, 7: 48}
 BY_BANKS_FROM = 7
 
@@ -46,6 +46,7 @@ def tile_mix_feat_tm_quad_silu_kernel(tc, x, w4_words, w4_scales, w8_words, w8_s
         planes = keep.tile([P, 2, M], U8, name="planes", align_bytes=64)
         b_cols = keep.tile([P, 2, 2 * PACK], F32, name="b_cols")
         ident = keep.tile([P, P], F32, name="ident")
+        warm = keep.tile([P, 1], F32, name="warm")
         bias = keep.tile([P, M], F32, name="bias")
 
         load_start = [sum(LOADS[:i]) for i in range(len(LOADS))]
@@ -67,9 +68,9 @@ def tile_mix_feat_tm_quad_silu_kernel(tc, x, w4_words, w4_scales, w8_words, w8_s
         def load_x(i):
             nc.sync.dma_start(out=raw[i][:], in_=x_rows[:, :, load_start[i] : load_start[i] + LOADS[i]])
 
-        def load_scales(feat, src):
+        def load_scales(queue, feat, src):
             for q in range(4):
-                nc.sync.dma_start(
+                queue.dma_start(
                     out=planes[32 * q : 32 * q + 4, feat, :].bitcast(I32),
                     in_=src[0, 4 * q : 4 * q + 4, :].bitcast(I32),
                 )
@@ -193,15 +194,16 @@ def tile_mix_feat_tm_quad_silu_kernel(tc, x, w4_words, w4_scales, w8_words, w8_s
                 finish_bank(i, 0)
                 finish_bank(i, 1)
 
-        nc.vector.memset(planes[:].rearrange("p f n -> p (f n)").bitcast(I32), 0)
+        nc.gpsimd.memset(planes[:].rearrange("p f n -> p (f n)").bitcast(I32), 0)
         nc.sync.dma_start(out=b_cols[:, :, 0:PACK], in_=b.rearrange("(h p c) -> p h c", h=2, c=PACK))
-        load_x(0)
         make_identity(nc, ident[:])
-        load_scales(LINEAR, w8_scales)
+        load_scales(nc.scalar, LINEAR, w8_scales)
+        nc.scalar.activation(out=warm[:], in_=ident[:, 0:1], func=ACT.Silu)
+        load_x(0)
         load_w8(0)
         load_x(1)
         load_w4(0)
-        load_scales(SQUARE, w4_scales)
+        load_scales(nc.sync, SQUARE, w4_scales)
         load_x(2)
         load_w8(1)
         load_w4(1)
@@ -227,38 +229,36 @@ def tile_mix_feat_tm_quad_silu_kernel(tc, x, w4_words, w4_scales, w8_words, w8_s
             square_scalar(c)
         for c in OWN_BUFFER:
             quantize_both(c)
-        nc.vector.tensor_copy(*bias_views(0))
-        nc.scalar.copy(*bias_views(1))
+        nc.scalar.copy(*bias_views(0))
         for feat in (LINEAR, SQUARE):
             for i in (0, 1):
                 one_pass(i, 0, feat)
         cast_vector(2)
         square_vector(2)
         square_scalar(2)
+        nc.scalar.copy(*bias_views(1))
         quantize_in_turn(2)
         cast_gpsimd(3)
         square_gpsimd(3)
-
+        square_scalar(3)
         for i in (2, 3):
             multiply(i, 0)
         for i in range(4):
             multiply(i, 1)
-        empty(0, 0)
-        finish_bank(0, 0)
-        square_scalar(3)
-        for i in (1, 2):
+        for i in range(3):
             empty(i, 0)
             finish_bank(i, 0)
+        square_scalar(4)
         empty(3, 0)
         for i in (0, 1):
             empty(i, 1)
             finish_bank(i, 1)
-        square_vector(4)
+        if 4 in VECTOR_SQUARES:
+            square_vector(4)
         quantize_in_turn(3)
         cast_gpsimd(4)
         square_gpsimd(5)
         multiply_tile(4)
-        square_scalar(4)
         empty(2, 1)
         finish_bank(2, 1)
         empty(3, 1)

@@ -29,8 +29,8 @@ CHUNKS = [128, 128, 256, 256, 256, 256, 128, 128]
 WIDE = max(CHUNKS)
 LAST = len(CHUNKS) - 1
 OWN_BUFFER = (0, 1)
-VECTOR_SQUARES = {2: 64, 4: 32, 5: 48}
-GPSIMD_SQUARES = {3: 96, 5: 48, 6: 48, 7: 48}
+VECTOR_SQUARES = {2: 64, 4: 32}
+GPSIMD_SQUARES = {3: 96, 5: 48, 6: 48, 7: 112}
 BY_BANKS_FROM = 7
 
 
@@ -68,9 +68,9 @@ def tile_mix_feat_tm_quad_silu_kernel(tc, x, w4_words, w4_scales, w8_words, w8_s
         def load_x(i):
             nc.sync.dma_start(out=raw[i][:], in_=x_rows[:, :, load_start[i] : load_start[i] + LOADS[i]])
 
-        def load_scales(queue, feat, src):
+        def load_scales(feat, src):
             for q in range(4):
-                queue.dma_start(
+                nc.sync.dma_start(
                     out=planes[32 * q : 32 * q + 4, feat, :].bitcast(I32),
                     in_=src[0, 4 * q : 4 * q + 4, :].bitcast(I32),
                 )
@@ -87,8 +87,7 @@ def tile_mix_feat_tm_quad_silu_kernel(tc, x, w4_words, w4_scales, w8_words, w8_s
         def feats(c):
             if c in OWN_BUFFER:
                 return own_feats[c][:]
-            xb_start = WIDE + (CHUNKS[c] if c == LAST else 0)
-            lo = (xb_start - place(c, LINEAR) * CHUNKS[c]) * PACK
+            lo = (WIDE - place(c, LINEAR) * CHUNKS[c]) * PACK
             return shared[:, lo : lo + 2 * CHUNKS[c] * PACK].rearrange("p (f t j) -> p f t j", f=2, j=PACK)
 
         def feature(c, feat):
@@ -110,8 +109,8 @@ def tile_mix_feat_tm_quad_silu_kernel(tc, x, w4_words, w4_scales, w8_words, w8_s
 
         def cast_gpsimd(c):
             nc.gpsimd.tensor_scalar(
-                out=shared[:, WIDE * PACK : 2 * WIDE * PACK].rearrange("p (t j) -> p t j", j=PACK),
-                in0=raw_tokens(c, 0, WIDE).rearrange("p j t -> p t j"),
+                out=feature(c, LINEAR),
+                in0=raw_tokens(c, 0, CHUNKS[c]).rearrange("p j t -> p t j"),
                 scalar1=1.0,
                 scalar2=0.0,
                 op0=ALU.mult,
@@ -141,8 +140,8 @@ def tile_mix_feat_tm_quad_silu_kernel(tc, x, w4_words, w4_scales, w8_words, w8_s
                 in_=feats(c).rearrange("p f t j -> p (f t j)"),
             )
 
-        def quantize_in_turn(c):
-            for feat in (LINEAR, SQUARE):
+        def quantize_in_turn(c, order=(LINEAR, SQUARE)):
+            for feat in order:
                 nc.vector.quantize_mx(
                     out=codes[c][:, place(c, feat), :].bitcast(FP8X4),
                     scales=scales[c][:, place(c, feat), :],
@@ -194,16 +193,16 @@ def tile_mix_feat_tm_quad_silu_kernel(tc, x, w4_words, w4_scales, w8_words, w8_s
                 finish_bank(i, 0)
                 finish_bank(i, 1)
 
-        nc.gpsimd.memset(planes[:].rearrange("p f n -> p (f n)").bitcast(I32), 0)
+        nc.vector.memset(planes[:].rearrange("p f n -> p (f n)").bitcast(I32), 0)
         nc.sync.dma_start(out=b_cols[:, :, 0:PACK], in_=b.rearrange("(h p c) -> p h c", h=2, c=PACK))
-        make_identity(nc, ident[:])
-        load_scales(nc.scalar, LINEAR, w8_scales)
-        nc.scalar.activation(out=warm[:], in_=ident[:, 0:1], func=ACT.Silu)
         load_x(0)
+        make_identity(nc, ident[:])
+        load_scales(LINEAR, w8_scales)
+        nc.scalar.activation(out=warm[:], in_=ident[:, 0:1], func=ACT.Silu)
         load_w8(0)
         load_x(1)
         load_w4(0)
-        load_scales(nc.sync, SQUARE, w4_scales)
+        load_scales(SQUARE, w4_scales)
         load_x(2)
         load_w8(1)
         load_w4(1)
@@ -280,14 +279,16 @@ def tile_mix_feat_tm_quad_silu_kernel(tc, x, w4_words, w4_scales, w8_words, w8_s
             finish_tile(i + 1)
             multiply_tile(i + 3)
 
-        for c in (LAST - 1, LAST):
-            i = chunk_start[c] // P
-            empty_tile(i - 2)
-            quantize_both(c)
-            if c < LAST:
-                square_scalar(LAST)
-            finish_tile(i - 2)
-            multiply_tile(i)
+        empty_tile(TILES - 4)
+        quantize_in_turn(LAST - 1)
+        cast_gpsimd(LAST)
+        square_scalar(LAST)
+        finish_tile(TILES - 4)
+        multiply_tile(TILES - 2)
+        empty_tile(TILES - 3)
+        quantize_in_turn(LAST, (SQUARE, LINEAR))
+        finish_tile(TILES - 3)
+        multiply_tile(TILES - 1)
         for i in (TILES - 2, TILES - 1):
             empty_tile(i)
             finish_tile(i)

@@ -29,9 +29,9 @@ CHUNKS = [128, 128, 256, 256, 256, 256, 128, 128]
 WIDE = max(CHUNKS)
 LAST = len(CHUNKS) - 1
 OWN_BUFFER = (0, 1)
-VECTOR_SQUARES = {2: 64, 4: 32}
+VECTOR_SQUARES = {2: 64, 4: 32, 5: 24}
 GPSIMD_SQUARES = {3: 96, 5: 48, 6: 48, 7: 112}
-BY_BANKS_FROM = 7
+BY_BANKS_FROM = 5
 
 
 def tile_mix_feat_tm_quad_silu_kernel(tc, x, w4_words, w4_scales, w8_words, w8_scales, b, out):
@@ -43,7 +43,7 @@ def tile_mix_feat_tm_quad_silu_kernel(tc, x, w4_words, w4_scales, w8_words, w8_s
 
         w8 = [keep.tile([P, BANK], U32, name="w8_%d" % h, align_bytes=64) for h in range(2)]
         w4 = [keep.tile([P, 2 * BANK], U8, name="w4_%d" % h, align_bytes=64) for h in range(2)]
-        planes = keep.tile([P, 2, M], U8, name="planes", align_bytes=64)
+        planes = [keep.tile([P, M], U8, name="plane%d" % f, align_bytes=64) for f in range(2)]
         b_cols = keep.tile([P, 2, 2 * PACK], F32, name="b_cols")
         ident = keep.tile([P, P], F32, name="ident")
         warm = keep.tile([P, 1], F32, name="warm")
@@ -58,7 +58,9 @@ def tile_mix_feat_tm_quad_silu_kernel(tc, x, w4_words, w4_scales, w8_words, w8_s
         shared = keep.tile([P, 3 * WIDE * PACK], BF16, name="shared", align_bytes=64)
         codes = [keep.tile([P, 2, w], U32, name="codes%d" % c, align_bytes=64) for c, w in enumerate(CHUNKS)]
         scales = [keep.tile([P, 2, w], U8, name="scales%d" % c, align_bytes=64) for c, w in enumerate(CHUNKS)]
-        res = [keep.tile([P, M], F32, name="res%d" % i) for i in range(TILES)]
+        results = keep.tile([P, TILES, M], F32, name="results")
+        res = [results[:, i, :] for i in range(TILES)]
+        out_tiles = out.rearrange("(i p) n -> p i n", p=P)
         acc = {}
 
         x_rows = x.rearrange("(p j) t -> p j t", j=PACK)
@@ -69,10 +71,10 @@ def tile_mix_feat_tm_quad_silu_kernel(tc, x, w4_words, w4_scales, w8_words, w8_s
             nc.sync.dma_start(out=raw[i][:], in_=x_rows[:, :, load_start[i] : load_start[i] + LOADS[i]])
 
         def load_scales(feat, src):
-            for q in range(4):
+            for r in range(4):
                 nc.sync.dma_start(
-                    out=planes[32 * q : 32 * q + 4, feat, :].bitcast(I32),
-                    in_=src[0, 4 * q : 4 * q + 4, :].bitcast(I32),
+                    out=planes[feat][r:P:32, :].bitcast(I32),
+                    in_=src[0, r:16:4, :].bitcast(I32),
                 )
 
         def load_w8(h):
@@ -148,24 +150,25 @@ def tile_mix_feat_tm_quad_silu_kernel(tc, x, w4_words, w4_scales, w8_words, w8_s
                     in_=feature(c, feat).rearrange("p t j -> p (t j)"),
                 )
 
-        def one_pass(i, h, feat):
+        def one_pass(i, h, feat, first=LINEAR):
             c = max(j for j in range(len(CHUNKS)) if chunk_start[j] <= i * P)
             cols = slice(i * P - chunk_start[c], (i + 1) * P - chunk_start[c])
-            if feat == LINEAR:
+            if feat == first:
                 acc[i, h] = psum.tile([P, BANK], F32, name="acc")
             nc.tensor.matmul_mx(
                 out=acc[i, h][:],
                 lhsT=codes[c][:, place(c, feat), cols].bitcast(FP8X4),
                 lhsT_scale=scales[c][:, place(c, feat), cols],
                 rhs=w8[h][:].bitcast(FP8X4) if feat == LINEAR else w4[h][:].bitcast(FP4X4),
-                rhs_scale=planes[:, feat, h * BANK : (h + 1) * BANK],
-                start=feat == LINEAR,
-                stop=feat == SQUARE,
+                rhs_scale=planes[feat][:, h * BANK : (h + 1) * BANK],
+                start=feat == first,
+                stop=feat != first,
             )
 
         def multiply(i, h):
-            one_pass(i, h, LINEAR)
-            one_pass(i, h, SQUARE)
+            first = SQUARE if i == TILES - 1 else LINEAR
+            one_pass(i, h, first, first)
+            one_pass(i, h, 1 - first, first)
 
         def multiply_tile(i):
             multiply(i, 0)
@@ -179,9 +182,15 @@ def tile_mix_feat_tm_quad_silu_kernel(tc, x, w4_words, w4_scales, w8_words, w8_s
             empty(i, 0)
             empty(i, 1)
 
-        def finish(i, lo, hi):
+        def activate(i, lo, hi):
             nc.scalar.activation(out=res[i][:, lo:hi], in_=res[i][:, lo:hi], func=ACT.Silu)
-            nc.sync.dma_start(out=out[i * P : (i + 1) * P, lo:hi], in_=res[i][:, lo:hi])
+
+        def store(first, last, lo, hi):
+            nc.sync.dma_start(out=out_tiles[:, first : last + 1, lo:hi], in_=results[:, first : last + 1, lo:hi])
+
+        def finish(i, lo, hi):
+            activate(i, lo, hi)
+            store(i, i, lo, hi)
 
         def finish_bank(i, h):
             finish(i, h * BANK, (h + 1) * BANK)
@@ -193,7 +202,8 @@ def tile_mix_feat_tm_quad_silu_kernel(tc, x, w4_words, w4_scales, w8_words, w8_s
                 finish_bank(i, 0)
                 finish_bank(i, 1)
 
-        nc.vector.memset(planes[:].rearrange("p f n -> p (f n)").bitcast(I32), 0)
+        for plane in planes:
+            nc.vector.memset(plane[:].bitcast(I32), 0)
         nc.sync.dma_start(out=b_cols[:, :, 0:PACK], in_=b.rearrange("(h p c) -> p h c", h=2, c=PACK))
         load_x(0)
         make_identity(nc, ident[:])
@@ -244,24 +254,26 @@ def tile_mix_feat_tm_quad_silu_kernel(tc, x, w4_words, w4_scales, w8_words, w8_s
             multiply(i, 0)
         for i in range(4):
             multiply(i, 1)
-        for i in range(3):
-            empty(i, 0)
-            finish_bank(i, 0)
+        for pair in ((0, 1), (2, 3)):
+            for i in pair:
+                empty(i, 0)
+                activate(i, 0, BANK)
+            store(*pair, 0, BANK)
         square_scalar(4)
-        empty(3, 0)
         for i in (0, 1):
             empty(i, 1)
-            finish_bank(i, 1)
+            activate(i, BANK, M)
+        store(0, 1, BANK, M)
         if 4 in VECTOR_SQUARES:
             square_vector(4)
         quantize_in_turn(3)
         cast_gpsimd(4)
         square_gpsimd(5)
         multiply_tile(4)
-        empty(2, 1)
-        finish_bank(2, 1)
-        empty(3, 1)
-        finish_tile(3)
+        for i in (2, 3):
+            empty(i, 1)
+            activate(i, BANK, M)
+        store(2, 3, BANK, M)
         multiply_tile(5)
 
         for c in (3, 4):

@@ -24,13 +24,13 @@ TILES = T // P
 RUN = 4
 LINEAR, SQUARE = 0, 1
 
-LOADS = [256, 256, 256, 256, 512]
+LOADS = [256, 256, 128, 128, 256, 512]
 CHUNKS = [128, 128, 256, 256, 256, 256, 128, 128]
 WIDE = max(CHUNKS)
 LAST = len(CHUNKS) - 1
 OWN_BUFFER = (0, 1)
-VECTOR_SQUARES = {2: 64, 4: 32, 5: 24}
-GPSIMD_SQUARES = {3: 96, 5: 48, 6: 48, 7: 112}
+VECTOR_SQUARES = {2: 48, 5: 32}
+GPSIMD_SQUARES = {4: 112, 6: 40, 7: 104}
 BY_BANKS_FROM = 5
 
 
@@ -96,7 +96,7 @@ def tile_mix_feat_tm_quad_silu_kernel(tc, x, w4_words, w4_scales, w8_words, w8_s
             return feats(c)[:, place(c, feat), :, :]
 
         def raw_tokens(c, lo, hi):
-            i = max(j for j in range(len(LOADS)) if load_start[j] <= chunk_start[c])
+            i = max(j for j in range(len(LOADS)) if load_start[j] <= chunk_start[c] + lo)
             t0 = chunk_start[c] - load_start[i]
             return raw[i][:, :, t0 + lo : t0 + hi]
 
@@ -109,10 +109,11 @@ def tile_mix_feat_tm_quad_silu_kernel(tc, x, w4_words, w4_scales, w8_words, w8_s
         def cast_vector(c):
             nc.vector.tensor_copy(out=feature_runs(c, LINEAR, 0, CHUNKS[c]), in_=raw_runs(c, 0, CHUNKS[c]))
 
-        def cast_gpsimd(c):
+        def cast_gpsimd(c, lo=0, hi=None):
+            hi = hi or CHUNKS[c]
             nc.gpsimd.tensor_scalar(
-                out=feature(c, LINEAR),
-                in0=raw_tokens(c, 0, CHUNKS[c]).rearrange("p j t -> p t j"),
+                out=feature(c, LINEAR)[:, lo:hi, :],
+                in0=raw_tokens(c, lo, hi).rearrange("p j t -> p t j"),
                 scalar1=1.0,
                 scalar2=0.0,
                 op0=ALU.mult,
@@ -185,6 +186,10 @@ def tile_mix_feat_tm_quad_silu_kernel(tc, x, w4_words, w4_scales, w8_words, w8_s
         def activate(i, lo, hi):
             nc.scalar.activation(out=res[i][:, lo:hi], in_=res[i][:, lo:hi], func=ACT.Silu)
 
+        def activate_pair(i, h):
+            both = results[:, i : i + 2, h * BANK : (h + 1) * BANK]
+            nc.scalar.activation(out=both, in_=both, func=ACT.Silu)
+
         def store(first, last, lo, hi):
             nc.sync.dma_start(out=out_tiles[:, first : last + 1, lo:hi], in_=results[:, first : last + 1, lo:hi])
 
@@ -214,10 +219,11 @@ def tile_mix_feat_tm_quad_silu_kernel(tc, x, w4_words, w4_scales, w8_words, w8_s
         load_w4(0)
         load_scales(SQUARE, w4_scales)
         load_x(2)
+        load_x(3)
         load_w8(1)
         load_w4(1)
-        load_x(3)
         load_x(4)
+        load_x(5)
 
         spread = []
         for h in range(2):
@@ -247,9 +253,9 @@ def tile_mix_feat_tm_quad_silu_kernel(tc, x, w4_words, w4_scales, w8_words, w8_s
         square_scalar(2)
         nc.scalar.copy(*bias_views(1))
         quantize_in_turn(2)
-        cast_gpsimd(3)
-        square_gpsimd(3)
-        square_scalar(3)
+        for lo in (0, P):
+            cast_gpsimd(3, lo, lo + P)
+            nc.scalar.activation(out=feature_runs(3, SQUARE, lo, lo + P), in_=raw_runs(3, lo, lo + P), func=ACT.Square)
         for i in (2, 3):
             multiply(i, 0)
         for i in range(4):
@@ -259,22 +265,18 @@ def tile_mix_feat_tm_quad_silu_kernel(tc, x, w4_words, w4_scales, w8_words, w8_s
                 empty(i, 0)
                 activate(i, 0, BANK)
             store(*pair, 0, BANK)
-        square_scalar(4)
-        for i in (0, 1):
-            empty(i, 1)
-            activate(i, BANK, M)
-        store(0, 1, BANK, M)
-        if 4 in VECTOR_SQUARES:
-            square_vector(4)
         quantize_in_turn(3)
         cast_gpsimd(4)
-        square_gpsimd(5)
+        square_gpsimd(4)
+        square_scalar(4)
         multiply_tile(4)
-        for i in (2, 3):
+        for i in (0, 2):
             empty(i, 1)
-            activate(i, BANK, M)
-        store(2, 3, BANK, M)
-        multiply_tile(5)
+            empty(i + 1, 1)
+            activate_pair(i, 1)
+            store(i, i + 1, BANK, M)
+            if i == 0:
+                multiply_tile(5)
 
         for c in (3, 4):
             i = chunk_start[c] // P

@@ -21,7 +21,7 @@ PACK = 4
 BANK = 512
 PSUM_BANKS = 8
 TILES = T // P
-RUN = 4
+RUN = 2
 LINEAR, SQUARE = 0, 1
 
 LOADS = [256, 256, 128, 128, 256, 512]
@@ -30,7 +30,7 @@ WIDE = max(CHUNKS)
 LAST = len(CHUNKS) - 1
 OWN_BUFFER = (0, 1)
 VECTOR_SQUARES = {2: 48, 5: 32}
-GPSIMD_SQUARES = {4: 112, 6: 40, 7: 104}
+GPSIMD_SQUARES = {4: 128, 6: 40, 7: 104}
 BY_BANKS_FROM = 5
 
 

@@ -19,26 +19,29 @@ ALU = mybir.AluOpType
 P = 128
 PACK = 4
 BANK = 512
-PSUM_BANKS = 8
 TILES = T // P
 RUN = 2
 LINEAR, SQUARE = 0, 1
 
 LOADS = [256, 256, 128, 128, 256, 512]
-CHUNKS = [128, 128, 256, 256, 256, 256, 128, 128]
-WIDE = max(CHUNKS)
+CHUNKS = [256, 256, 256, 256, 256, 128, 128]
 LAST = len(CHUNKS) - 1
-OWN_BUFFER = (0, 1)
-VECTOR_SQUARES = {2: 48, 5: 32}
-GPSIMD_SQUARES = {4: 128, 6: 40, 7: 104}
-BY_BANKS_FROM = 5
+VECTOR_SQUARES = {1: 48}
+GPSIMD_SQUARES = {3: 112, 5: 32, 6: 96}
+BY_BANKS_FROM = 7
+FOLLOW_FROM = 9
+OPEN_BANKS = 5
+IN_ORDER = (0, 1, 6, 8, 10, 11)
+QUANTISE_AFTER = {2: 4, 3: 10, 4: 14, 5: 18, 6: 20}
+SCALAR_SQUARES_AT = {1: (2,), 6: (3,), 12: (4,), 16: (5,), 18: (6,)}
+GPSIMD_SQUARES_AFTER = {3: 3, 4: 5, 5: 6}
 
 
 def tile_mix_feat_tm_quad_silu_kernel(tc, x, w4_words, w4_scales, w8_words, w8_scales, b, out):
     nc = tc.nc
     with ExitStack() as ctx:
         keep = ctx.enter_context(tc.tile_pool(name="keep", bufs=1))
-        psum = ctx.enter_context(tc.psum_pool(name="psum", bufs=PSUM_BANKS))
+        psum = ctx.enter_context(tc.psum_pool(name="psum", bufs=OPEN_BANKS))
         ctx.enter_context(tc.manual_schedule())
 
         w8 = [keep.tile([P, BANK], U32, name="w8_%d" % h, align_bytes=64) for h in range(2)]
@@ -52,14 +55,11 @@ def tile_mix_feat_tm_quad_silu_kernel(tc, x, w4_words, w4_scales, w8_words, w8_s
         load_start = [sum(LOADS[:i]) for i in range(len(LOADS))]
         raw = [keep.tile([P, PACK, w], F32, name="raw%d" % i) for i, w in enumerate(LOADS)]
         chunk_start = [sum(CHUNKS[:c]) for c in range(len(CHUNKS))]
-        own_feats = {
-            c: keep.tile([P, 2, CHUNKS[c], PACK], BF16, name="feats%d" % c, align_bytes=64) for c in OWN_BUFFER
-        }
-        shared = keep.tile([P, 3 * WIDE * PACK], BF16, name="shared", align_bytes=64)
+        xb = keep.tile([P, max(CHUNKS) * PACK], BF16, name="xb", align_bytes=64)
+        xa = [keep.tile([P, w * PACK], BF16, name="xa%d" % c, align_bytes=64) for c, w in enumerate(CHUNKS)]
         codes = [keep.tile([P, 2, w], U32, name="codes%d" % c, align_bytes=64) for c, w in enumerate(CHUNKS)]
         scales = [keep.tile([P, 2, w], U8, name="scales%d" % c, align_bytes=64) for c, w in enumerate(CHUNKS)]
         results = keep.tile([P, TILES, M], F32, name="results")
-        res = [results[:, i, :] for i in range(TILES)]
         out_tiles = out.rearrange("(i p) n -> p i n", p=P)
         acc = {}
 
@@ -72,10 +72,7 @@ def tile_mix_feat_tm_quad_silu_kernel(tc, x, w4_words, w4_scales, w8_words, w8_s
 
         def load_scales(feat, src):
             for r in range(4):
-                nc.sync.dma_start(
-                    out=planes[feat][r:P:32, :].bitcast(I32),
-                    in_=src[0, r:16:4, :].bitcast(I32),
-                )
+                nc.sync.dma_start(out=planes[feat][r:P:32, :].bitcast(I32), in_=src[0, r:16:4, :].bitcast(I32))
 
         def load_w8(h):
             nc.sync.dma_start(out=w8[h][:].bitcast(I32), in_=w8_src[:, h * BANK : (h + 1) * BANK])
@@ -83,17 +80,11 @@ def tile_mix_feat_tm_quad_silu_kernel(tc, x, w4_words, w4_scales, w8_words, w8_s
         def load_w4(h):
             nc.sync.dma_start(out=w4[h][:].bitcast(I32), in_=w4_src[:, h * BANK // 2 : (h + 1) * BANK // 2])
 
-        def place(c, feat):
-            return feat if c in OWN_BUFFER or c % 2 else 1 - feat
+        def flat(c, feat):
+            return xb[:, 0 : CHUNKS[c] * PACK] if feat == LINEAR else xa[c][:]
 
-        def feats(c):
-            if c in OWN_BUFFER:
-                return own_feats[c][:]
-            lo = (WIDE - place(c, LINEAR) * CHUNKS[c]) * PACK
-            return shared[:, lo : lo + 2 * CHUNKS[c] * PACK].rearrange("p (f t j) -> p f t j", f=2, j=PACK)
-
-        def feature(c, feat):
-            return feats(c)[:, place(c, feat), :, :]
+        def feature(c, feat, lo, hi):
+            return flat(c, feat).rearrange("p (t j) -> p t j", j=PACK)[:, lo:hi, :]
 
         def raw_tokens(c, lo, hi):
             i = max(j for j in range(len(LOADS)) if load_start[j] <= chunk_start[c] + lo)
@@ -104,21 +95,25 @@ def tile_mix_feat_tm_quad_silu_kernel(tc, x, w4_words, w4_scales, w8_words, w8_s
             return raw_tokens(c, lo, hi).rearrange("p j (g i) -> p g j i", i=RUN)
 
         def feature_runs(c, feat, lo, hi):
-            return feature(c, feat)[:, lo:hi, :].rearrange("p (g i) j -> p g j i", i=RUN)
+            return feature(c, feat, lo, hi).rearrange("p (g i) j -> p g j i", i=RUN)
+
+        def by_load(c, lo, hi):
+            cuts = [t - chunk_start[c] for t in load_start if lo < t - chunk_start[c] < hi]
+            return zip([lo] + cuts, cuts + [hi])
 
         def cast_vector(c):
             nc.vector.tensor_copy(out=feature_runs(c, LINEAR, 0, CHUNKS[c]), in_=raw_runs(c, 0, CHUNKS[c]))
 
-        def cast_gpsimd(c, lo=0, hi=None):
-            hi = hi or CHUNKS[c]
-            nc.gpsimd.tensor_scalar(
-                out=feature(c, LINEAR)[:, lo:hi, :],
-                in0=raw_tokens(c, lo, hi).rearrange("p j t -> p t j"),
-                scalar1=1.0,
-                scalar2=0.0,
-                op0=ALU.mult,
-                op1=ALU.add,
-            )
+        def cast_gpsimd(c):
+            for lo, hi in by_load(c, 0, CHUNKS[c]):
+                nc.gpsimd.tensor_scalar(
+                    out=feature(c, LINEAR, lo, hi),
+                    in0=raw_tokens(c, lo, hi).rearrange("p j t -> p t j"),
+                    scalar1=1.0,
+                    scalar2=0.0,
+                    op0=ALU.mult,
+                    op1=ALU.add,
+                )
 
         def square_vector(c):
             src = raw_runs(c, 0, VECTOR_SQUARES[c])
@@ -128,28 +123,18 @@ def tile_mix_feat_tm_quad_silu_kernel(tc, x, w4_words, w4_scales, w8_words, w8_s
             lo = VECTOR_SQUARES.get(c, 0)
             hi = lo + GPSIMD_SQUARES[c]
             src = raw_tokens(c, lo, hi).rearrange("p j t -> p t j")
-            nc.gpsimd.tensor_tensor(out=feature(c, SQUARE)[:, lo:hi, :], in0=src, in1=src, op=ALU.mult)
+            nc.gpsimd.tensor_tensor(out=feature(c, SQUARE, lo, hi), in0=src, in1=src, op=ALU.mult)
 
         def square_scalar(c):
-            lo = VECTOR_SQUARES.get(c, 0) + GPSIMD_SQUARES.get(c, 0)
-            nc.scalar.activation(
-                out=feature_runs(c, SQUARE, lo, CHUNKS[c]), in_=raw_runs(c, lo, CHUNKS[c]), func=ACT.Square
-            )
+            for lo, hi in by_load(c, VECTOR_SQUARES.get(c, 0) + GPSIMD_SQUARES.get(c, 0), CHUNKS[c]):
+                nc.scalar.activation(out=feature_runs(c, SQUARE, lo, hi), in_=raw_runs(c, lo, hi), func=ACT.Square)
 
-        def quantize_both(c):
-            nc.vector.quantize_mx(
-                out=codes[c][:].rearrange("p f t -> p (f t)").bitcast(FP8X4),
-                scales=scales[c][:].rearrange("p f t -> p (f t)"),
-                in_=feats(c).rearrange("p f t j -> p (f t j)"),
-            )
+        def quantize(c, feat):
+            nc.vector.quantize_mx(out=codes[c][:, feat, :].bitcast(FP8X4), scales=scales[c][:, feat, :], in_=flat(c, feat))
 
-        def quantize_in_turn(c, order=(LINEAR, SQUARE)):
+        def quantize_both(c, order=(LINEAR, SQUARE)):
             for feat in order:
-                nc.vector.quantize_mx(
-                    out=codes[c][:, place(c, feat), :].bitcast(FP8X4),
-                    scales=scales[c][:, place(c, feat), :],
-                    in_=feature(c, feat).rearrange("p t j -> p (t j)"),
-                )
+                quantize(c, feat)
 
         def one_pass(i, h, feat, first=LINEAR):
             c = max(j for j in range(len(CHUNKS)) if chunk_start[j] <= i * P)
@@ -158,8 +143,8 @@ def tile_mix_feat_tm_quad_silu_kernel(tc, x, w4_words, w4_scales, w8_words, w8_s
                 acc[i, h] = psum.tile([P, BANK], F32, name="acc")
             nc.tensor.matmul_mx(
                 out=acc[i, h][:],
-                lhsT=codes[c][:, place(c, feat), cols].bitcast(FP8X4),
-                lhsT_scale=scales[c][:, place(c, feat), cols],
+                lhsT=codes[c][:, feat, cols].bitcast(FP8X4),
+                lhsT_scale=scales[c][:, feat, cols],
                 rhs=w8[h][:].bitcast(FP8X4) if feat == LINEAR else w4[h][:].bitcast(FP4X4),
                 rhs_scale=planes[feat][:, h * BANK : (h + 1) * BANK],
                 start=feat == first,
@@ -171,41 +156,33 @@ def tile_mix_feat_tm_quad_silu_kernel(tc, x, w4_words, w4_scales, w8_words, w8_s
             one_pass(i, h, first, first)
             one_pass(i, h, 1 - first, first)
 
-        def multiply_tile(i):
-            multiply(i, 0)
-            multiply(i, 1)
-
         def empty(i, h):
             n = slice(h * BANK, (h + 1) * BANK)
-            nc.vector.tensor_tensor(out=res[i][:, n], in0=acc[i, h][:], in1=bias[:, n], op=ALU.add)
+            nc.vector.tensor_tensor(out=results[:, i, n], in0=acc[i, h][:], in1=bias[:, n], op=ALU.add)
 
-        def empty_tile(i):
-            empty(i, 0)
-            empty(i, 1)
-
-        def activate(i, lo, hi):
-            nc.scalar.activation(out=res[i][:, lo:hi], in_=res[i][:, lo:hi], func=ACT.Silu)
-
-        def activate_pair(i, h):
-            both = results[:, i : i + 2, h * BANK : (h + 1) * BANK]
-            nc.scalar.activation(out=both, in_=both, func=ACT.Silu)
+        def activate(first, last, lo, hi):
+            part = results[:, first : last + 1, lo:hi]
+            nc.scalar.activation(out=part, in_=part, func=ACT.Silu)
 
         def store(first, last, lo, hi):
             nc.sync.dma_start(out=out_tiles[:, first : last + 1, lo:hi], in_=results[:, first : last + 1, lo:hi])
 
-        def finish(i, lo, hi):
-            activate(i, lo, hi)
-            store(i, i, lo, hi)
-
-        def finish_bank(i, h):
-            finish(i, h * BANK, (h + 1) * BANK)
-
-        def finish_tile(i):
+        def finish_pair(n, pair):
+            (i, h), (last, last_h) = pair
             if i < BY_BANKS_FROM:
-                finish(i, 0, M)
+                parts = [(h * BANK, (last_h + 1) * BANK)]
+            elif (n in IN_ORDER) == (i >= FOLLOW_FROM):
+                parts = [(0, BANK), (BANK, M)]
             else:
-                finish_bank(i, 0)
-                finish_bank(i, 1)
+                parts = [(BANK, M), (0, BANK)]
+            for lo, hi in parts:
+                activate(i, last, lo, hi)
+                store(i, last, lo, hi)
+
+        def prepare_gpsimd(c):
+            cast_gpsimd(c)
+            if c in GPSIMD_SQUARES_AFTER:
+                square_gpsimd(GPSIMD_SQUARES_AFTER[c])
 
         for plane in planes:
             nc.vector.memset(plane[:].bitcast(I32), 0)
@@ -218,12 +195,12 @@ def tile_mix_feat_tm_quad_silu_kernel(tc, x, w4_words, w4_scales, w8_words, w8_s
         load_x(1)
         load_w4(0)
         load_scales(SQUARE, w4_scales)
-        load_x(2)
-        load_x(3)
+        for i in range(2, len(LOADS) - 2):
+            load_x(i)
         load_w8(1)
         load_w4(1)
-        load_x(4)
-        load_x(5)
+        load_x(len(LOADS) - 2)
+        load_x(len(LOADS) - 1)
 
         spread = []
         for h in range(2):
@@ -233,76 +210,55 @@ def tile_mix_feat_tm_quad_silu_kernel(tc, x, w4_words, w4_scales, w8_words, w8_s
                 nc.tensor.transpose(bank[:, c * P : (c + 1) * P], col.to_broadcast([P, P]), ident[:])
             spread.append(bank)
 
-        def bias_views(h):
-            return (
+        def copy_bias(h):
+            nc.scalar.copy(
                 bias[:, h * BANK : (h + 1) * BANK].rearrange("q (p c) -> q p c", c=PACK),
                 spread[h][:].rearrange("q (c p) -> q p c", c=PACK),
             )
 
-        for c in OWN_BUFFER:
-            cast_vector(c)
-            square_scalar(c)
-        for c in OWN_BUFFER:
-            quantize_both(c)
-        nc.scalar.copy(*bias_views(0))
+        cast_vector(0)
+        square_scalar(0)
+        quantize_both(0)
+        copy_bias(0)
         for feat in (LINEAR, SQUARE):
             for i in (0, 1):
                 one_pass(i, 0, feat)
-        cast_vector(2)
-        square_vector(2)
-        square_scalar(2)
-        nc.scalar.copy(*bias_views(1))
-        quantize_in_turn(2)
-        for lo in (0, P):
-            cast_gpsimd(3, lo, lo + P)
-            nc.scalar.activation(out=feature_runs(3, SQUARE, lo, lo + P), in_=raw_runs(3, lo, lo + P), func=ACT.Square)
-        for i in (2, 3):
-            multiply(i, 0)
-        for i in range(4):
-            multiply(i, 1)
-        for pair in ((0, 1), (2, 3)):
-            for i in pair:
-                empty(i, 0)
-                activate(i, 0, BANK)
-            store(*pair, 0, BANK)
-        quantize_in_turn(3)
-        cast_gpsimd(4)
-        square_gpsimd(4)
-        square_scalar(4)
-        multiply_tile(4)
-        for i in (0, 2):
-            empty(i, 1)
-            empty(i + 1, 1)
-            activate_pair(i, 1)
-            store(i, i + 1, BANK, M)
-            if i == 0:
-                multiply_tile(5)
+        cast_vector(1)
+        square_vector(1)
+        square_scalar(1)
+        copy_bias(1)
+        quantize_both(1)
 
-        for c in (3, 4):
-            i = chunk_start[c] // P
-            empty_tile(i)
-            if c + 2 in VECTOR_SQUARES:
-                square_vector(c + 2)
-            quantize_in_turn(c + 1)
-            cast_gpsimd(c + 2)
-            square_gpsimd(c + 3)
-            finish_tile(i)
-            square_scalar(c + 2)
-            multiply_tile(i + 2)
-            empty_tile(i + 1)
-            finish_tile(i + 1)
-            multiply_tile(i + 3)
+        pairs = [[(i, h), (i + 1, h)] for h in range(2) for i in (0, 2)]
+        pairs.extend([(i, 0), (i, 1)] for i in range(4, TILES))
+        banks = [bank for pair in pairs for bank in pair]
+        emptied = []
 
-        empty_tile(TILES - 4)
-        quantize_in_turn(LAST - 1)
-        cast_gpsimd(LAST)
-        square_scalar(LAST)
-        finish_tile(TILES - 4)
-        multiply_tile(TILES - 2)
-        empty_tile(TILES - 3)
-        quantize_in_turn(LAST, (SQUARE, LINEAR))
-        finish_tile(TILES - 3)
-        multiply_tile(TILES - 1)
-        for i in (TILES - 2, TILES - 1):
-            empty_tile(i)
-            finish_tile(i)
+        def multiply_ready(c):
+            tokens = chunk_start[c] if c <= LAST else T
+            for n, (i, h) in enumerate(banks):
+                free = n < OPEN_BANKS or banks[n - OPEN_BANKS] in emptied
+                if i * P >= tokens or not free:
+                    return
+                if (i, h) not in acc:
+                    multiply(i, h)
+
+        chunk = 2
+        prepare_gpsimd(chunk)
+        multiply_ready(chunk)
+        for n, pair in enumerate(pairs):
+            for i, h in pair if n in IN_ORDER else reversed(pair):
+                empty(i, h)
+                emptied.append((i, h))
+                multiply_ready(chunk)
+                for c in SCALAR_SQUARES_AT.get(len(emptied), ()):
+                    square_scalar(c)
+                if len(emptied) == QUANTISE_AFTER.get(chunk):
+                    if chunk + 1 in VECTOR_SQUARES:
+                        square_vector(chunk + 1)
+                    quantize_both(chunk, (SQUARE, LINEAR) if chunk == LAST else (LINEAR, SQUARE))
+                    chunk = chunk + 1
+                    multiply_ready(chunk)
+                    if chunk <= LAST:
+                        prepare_gpsimd(chunk)
+            finish_pair(n, pair)

@@ -20,18 +20,17 @@ P = 128
 PACK = 4
 BANK = 512
 TILES = T // P
+BURST = 256
 RUN = 2
 LINEAR, SQUARE = 0, 1
 
 LOADS = [256, 256, 128, 128, 256, 512]
 CHUNKS = [256, 256, 256, 256, 256, 128, 128]
 LAST = len(CHUNKS) - 1
-VECTOR_SQUARES = {1: 48}
-GPSIMD_SQUARES = {3: 112, 5: 32, 6: 96}
-BY_BANKS_FROM = 7
-FOLLOW_FROM = 9
-OPEN_BANKS = 5
-IN_ORDER = (0, 1, 6, 8, 10, 11)
+VECTOR_SQUARES = {1: 48, 4: 32}
+GPSIMD_SQUARES = {3: 128, 5: 40, 6: 104}
+BY_BANKS_FROM = 5
+OPEN_BANKS = 8
 QUANTISE_AFTER = {2: 4, 3: 10, 4: 14, 5: 18, 6: 20}
 SCALAR_SQUARES_AT = {1: (2,), 6: (3,), 12: (4,), 16: (5,), 18: (6,)}
 GPSIMD_SQUARES_AFTER = {3: 3, 4: 5, 5: 6}
@@ -44,22 +43,22 @@ def tile_mix_feat_tm_quad_silu_kernel(tc, x, w4_words, w4_scales, w8_words, w8_s
         psum = ctx.enter_context(tc.psum_pool(name="psum", bufs=OPEN_BANKS))
         ctx.enter_context(tc.manual_schedule())
 
-        w8 = [keep.tile([P, BANK], U32, name="w8_%d" % h, align_bytes=64) for h in range(2)]
-        w4 = [keep.tile([P, 2 * BANK], U8, name="w4_%d" % h, align_bytes=64) for h in range(2)]
-        planes = [keep.tile([P, M], U8, name="plane%d" % f, align_bytes=64) for f in range(2)]
+        w8 = [keep.tile([P, BANK], U32, name="w8_%d" % h, align_bytes=BURST) for h in range(2)]
+        w4 = [keep.tile([P, 2 * BANK], U8, name="w4_%d" % h, align_bytes=BURST) for h in range(2)]
+        planes = [keep.tile([P, M], U8, name="plane%d" % f, align_bytes=BURST) for f in range(2)]
         b_cols = keep.tile([P, 2, 2 * PACK], F32, name="b_cols")
         ident = keep.tile([P, P], F32, name="ident")
         warm = keep.tile([P, 1], F32, name="warm")
         bias = keep.tile([P, M], F32, name="bias")
 
         load_start = [sum(LOADS[:i]) for i in range(len(LOADS))]
-        raw = [keep.tile([P, PACK, w], F32, name="raw%d" % i) for i, w in enumerate(LOADS)]
+        raw = [keep.tile([P, PACK, w], F32, name="raw%d" % i, align_bytes=BURST) for i, w in enumerate(LOADS)]
         chunk_start = [sum(CHUNKS[:c]) for c in range(len(CHUNKS))]
         xb = keep.tile([P, max(CHUNKS) * PACK], BF16, name="xb", align_bytes=64)
         xa = [keep.tile([P, w * PACK], BF16, name="xa%d" % c, align_bytes=64) for c, w in enumerate(CHUNKS)]
         codes = [keep.tile([P, 2, w], U32, name="codes%d" % c, align_bytes=64) for c, w in enumerate(CHUNKS)]
         scales = [keep.tile([P, 2, w], U8, name="scales%d" % c, align_bytes=64) for c, w in enumerate(CHUNKS)]
-        results = keep.tile([P, TILES, M], F32, name="results")
+        results = keep.tile([P, TILES, M], F32, name="results", align_bytes=BURST)
         out_tiles = out.rearrange("(i p) n -> p i n", p=P)
         acc = {}
 
@@ -171,10 +170,8 @@ def tile_mix_feat_tm_quad_silu_kernel(tc, x, w4_words, w4_scales, w8_words, w8_s
             (i, h), (last, last_h) = pair
             if i < BY_BANKS_FROM:
                 parts = [(h * BANK, (last_h + 1) * BANK)]
-            elif (n in IN_ORDER) == (i >= FOLLOW_FROM):
-                parts = [(0, BANK), (BANK, M)]
             else:
-                parts = [(BANK, M), (0, BANK)]
+                parts = [(0, BANK), (BANK, M)]
             for lo, hi in parts:
                 activate(i, last, lo, hi)
                 store(i, last, lo, hi)
@@ -247,7 +244,7 @@ def tile_mix_feat_tm_quad_silu_kernel(tc, x, w4_words, w4_scales, w8_words, w8_s
         prepare_gpsimd(chunk)
         multiply_ready(chunk)
         for n, pair in enumerate(pairs):
-            for i, h in pair if n in IN_ORDER else reversed(pair):
+            for i, h in pair:
                 empty(i, h)
                 emptied.append((i, h))
                 multiply_ready(chunk)

@@ -27,8 +27,8 @@ LINEAR, SQUARE = 0, 1
 LOADS = [256, 256, 128, 128, 256, 512]
 CHUNKS = [256, 256, 256, 256, 256, 128, 128]
 LAST = len(CHUNKS) - 1
-VECTOR_SQUARES = {1: 48, 4: 32}
-GPSIMD_SQUARES = {3: 128, 5: 40, 6: 104}
+VECTOR_SQUARES = {1: 48}
+GPSIMD_SQUARES = {3: 152, 5: 64, 6: 120}
 BY_BANKS_FROM = 5
 OPEN_BANKS = 8
 QUANTISE_AFTER = {2: 4, 3: 10, 4: 14, 5: 18, 6: 20}
@@ -106,8 +106,8 @@ def tile_mix_feat_tm_quad_silu_kernel(tc, x, w4_words, w4_scales, w8_words, w8_s
         def cast_gpsimd(c):
             for lo, hi in by_load(c, 0, CHUNKS[c]):
                 nc.gpsimd.tensor_scalar(
-                    out=feature(c, LINEAR, lo, hi),
-                    in0=raw_tokens(c, lo, hi).rearrange("p j t -> p t j"),
+                    out=feature_runs(c, LINEAR, lo, hi),
+                    in0=raw_runs(c, lo, hi),
                     scalar1=1.0,
                     scalar2=0.0,
                     op0=ALU.mult,
@@ -121,8 +121,8 @@ def tile_mix_feat_tm_quad_silu_kernel(tc, x, w4_words, w4_scales, w8_words, w8_s
         def square_gpsimd(c):
             lo = VECTOR_SQUARES.get(c, 0)
             hi = lo + GPSIMD_SQUARES[c]
-            src = raw_tokens(c, lo, hi).rearrange("p j t -> p t j")
-            nc.gpsimd.tensor_tensor(out=feature(c, SQUARE, lo, hi), in0=src, in1=src, op=ALU.mult)
+            src = raw_runs(c, lo, hi)
+            nc.gpsimd.tensor_tensor(out=feature_runs(c, SQUARE, lo, hi), in0=src, in1=src, op=ALU.mult)
 
         def square_scalar(c):
             for lo, hi in by_load(c, VECTOR_SQUARES.get(c, 0) + GPSIMD_SQUARES.get(c, 0), CHUNKS[c]):

@@ -23,17 +23,20 @@ TILES = T // P
 BURST = 256
 RUN = 2
 LINEAR, SQUARE = 0, 1
+OPEN_BANKS = 8
 
 LOADS = [256, 256, 128, 128, 256, 512]
 CHUNKS = [256, 256, 256, 256, 256, 128, 128]
-LAST = len(CHUNKS) - 1
-VECTOR_SQUARES = {1: 48}
-GPSIMD_SQUARES = {3: 152, 5: 64, 6: 120}
-BY_BANKS_FROM = 5
-OPEN_BANKS = 8
-QUANTISE_AFTER = {2: 4, 3: 10, 4: 14, 5: 18, 6: 20}
-SCALAR_SQUARES_AT = {1: (2,), 6: (3,), 12: (4,), 16: (5,), 18: (6,)}
-GPSIMD_SQUARES_AFTER = {3: 3, 4: 5, 5: 6}
+VECTOR_SQUARES = 48
+GPSIMD_SQUARES = {3: [(3, 128, 256), (4, 176, 256)], 4: [(4, 128, 176)], 5: [(6, 24, 128)]}
+SCALAR_SQUARES = {1: (2, 0, 256), 3: (3, 0, 128), 11: (4, 0, 128), 15: (5, 0, 128), 17: (6, 0, 24)}
+QUANTISE_AFTER = {2: 2, 3: 10, 4: 14, 5: 18, 6: 20}
+SQUARES_FIRST = (2, 6)
+SILU_BANKS = 1
+LOW_FIRST = 6
+BANKS = [(i, h) for h in range(2) for i in range(LOW_FIRST)] + [(i, h) for i in range(LOW_FIRST, TILES) for h in range(2)]
+PAIRS = range(0, 14, 2)
+STORES = [BANKS[n : n + 2] if n in PAIRS else BANKS[n : n + 1] for n in range(len(BANKS)) if n - 1 not in PAIRS]
 
 
 def tile_mix_feat_tm_quad_silu_kernel(tc, x, w4_words, w4_scales, w8_words, w8_scales, b, out):
@@ -53,7 +56,7 @@ def tile_mix_feat_tm_quad_silu_kernel(tc, x, w4_words, w4_scales, w8_words, w8_s
 
         load_start = [sum(LOADS[:i]) for i in range(len(LOADS))]
         raw = [keep.tile([P, PACK, w], F32, name="raw%d" % i, align_bytes=BURST) for i, w in enumerate(LOADS)]
-        chunk_start = [sum(CHUNKS[:c]) for c in range(len(CHUNKS))]
+        chunk_start = [sum(CHUNKS[:c]) for c in range(len(CHUNKS) + 1)]
         xb = keep.tile([P, max(CHUNKS) * PACK], BF16, name="xb", align_bytes=64)
         xa = [keep.tile([P, w * PACK], BF16, name="xa%d" % c, align_bytes=64) for c, w in enumerate(CHUNKS)]
         codes = [keep.tile([P, 2, w], U32, name="codes%d" % c, align_bytes=64) for c, w in enumerate(CHUNKS)]
@@ -82,26 +85,21 @@ def tile_mix_feat_tm_quad_silu_kernel(tc, x, w4_words, w4_scales, w8_words, w8_s
         def flat(c, feat):
             return xb[:, 0 : CHUNKS[c] * PACK] if feat == LINEAR else xa[c][:]
 
-        def feature(c, feat, lo, hi):
-            return flat(c, feat).rearrange("p (t j) -> p t j", j=PACK)[:, lo:hi, :]
-
-        def raw_tokens(c, lo, hi):
+        def raw_runs(c, lo, hi):
             i = max(j for j in range(len(LOADS)) if load_start[j] <= chunk_start[c] + lo)
             t0 = chunk_start[c] - load_start[i]
-            return raw[i][:, :, t0 + lo : t0 + hi]
-
-        def raw_runs(c, lo, hi):
-            return raw_tokens(c, lo, hi).rearrange("p j (g i) -> p g j i", i=RUN)
+            return raw[i][:, :, t0 + lo : t0 + hi].rearrange("p j (g i) -> p g j i", i=RUN)
 
         def feature_runs(c, feat, lo, hi):
-            return feature(c, feat, lo, hi).rearrange("p (g i) j -> p g j i", i=RUN)
+            words = flat(c, feat).rearrange("p (t j) -> p t j", j=PACK)
+            return words[:, lo:hi, :].rearrange("p (g i) j -> p g j i", i=RUN)
 
         def by_load(c, lo, hi):
             cuts = [t - chunk_start[c] for t in load_start if lo < t - chunk_start[c] < hi]
             return zip([lo] + cuts, cuts + [hi])
 
-        def cast_vector(c):
-            nc.vector.tensor_copy(out=feature_runs(c, LINEAR, 0, CHUNKS[c]), in_=raw_runs(c, 0, CHUNKS[c]))
+        def cast_vector(c, lo, hi):
+            nc.vector.tensor_copy(out=feature_runs(c, LINEAR, lo, hi), in_=raw_runs(c, lo, hi))
 
         def cast_gpsimd(c):
             for lo, hi in by_load(c, 0, CHUNKS[c]):
@@ -114,29 +112,30 @@ def tile_mix_feat_tm_quad_silu_kernel(tc, x, w4_words, w4_scales, w8_words, w8_s
                     op1=ALU.add,
                 )
 
-        def square_vector(c):
-            src = raw_runs(c, 0, VECTOR_SQUARES[c])
-            nc.vector.tensor_tensor(out=feature_runs(c, SQUARE, 0, VECTOR_SQUARES[c]), in0=src, in1=src, op=ALU.mult)
-
-        def square_gpsimd(c):
-            lo = VECTOR_SQUARES.get(c, 0)
-            hi = lo + GPSIMD_SQUARES[c]
+        def square_two_inputs(engine, c, lo, hi):
             src = raw_runs(c, lo, hi)
-            nc.gpsimd.tensor_tensor(out=feature_runs(c, SQUARE, lo, hi), in0=src, in1=src, op=ALU.mult)
+            engine.tensor_tensor(out=feature_runs(c, SQUARE, lo, hi), in0=src, in1=src, op=ALU.mult)
 
-        def square_scalar(c):
-            for lo, hi in by_load(c, VECTOR_SQUARES.get(c, 0) + GPSIMD_SQUARES.get(c, 0), CHUNKS[c]):
+        def square_scalar(c, start, stop):
+            for lo, hi in by_load(c, start, stop):
                 nc.scalar.activation(out=feature_runs(c, SQUARE, lo, hi), in_=raw_runs(c, lo, hi), func=ACT.Square)
 
-        def quantize(c, feat):
-            nc.vector.quantize_mx(out=codes[c][:, feat, :].bitcast(FP8X4), scales=scales[c][:, feat, :], in_=flat(c, feat))
+        def quantize(c, feat, lo=0, hi=None):
+            cols = slice(lo, hi or CHUNKS[c])
+            nc.vector.quantize_mx(
+                out=codes[c][:, feat, cols].bitcast(FP8X4),
+                scales=scales[c][:, feat, cols],
+                in_=flat(c, feat)[:, cols.start * PACK : cols.stop * PACK],
+            )
 
-        def quantize_both(c, order=(LINEAR, SQUARE)):
-            for feat in order:
-                quantize(c, feat)
+        def chunk_of(i):
+            return max(j for j in range(len(CHUNKS)) if chunk_start[j] <= i * P)
+
+        def order(c):
+            return (SQUARE, LINEAR) if c in SQUARES_FIRST else (LINEAR, SQUARE)
 
         def one_pass(i, h, feat, first=LINEAR):
-            c = max(j for j in range(len(CHUNKS)) if chunk_start[j] <= i * P)
+            c = chunk_of(i)
             cols = slice(i * P - chunk_start[c], (i + 1) * P - chunk_start[c])
             if feat == first:
                 acc[i, h] = psum.tile([P, BANK], F32, name="acc")
@@ -151,35 +150,25 @@ def tile_mix_feat_tm_quad_silu_kernel(tc, x, w4_words, w4_scales, w8_words, w8_s
             )
 
         def multiply(i, h):
-            first = SQUARE if i == TILES - 1 else LINEAR
+            first, second = order(chunk_of(i))
             one_pass(i, h, first, first)
-            one_pass(i, h, 1 - first, first)
+            one_pass(i, h, second, first)
 
         def empty(i, h):
             n = slice(h * BANK, (h + 1) * BANK)
             nc.vector.tensor_tensor(out=results[:, i, n], in0=acc[i, h][:], in1=bias[:, n], op=ALU.add)
 
-        def activate(first, last, lo, hi):
-            part = results[:, first : last + 1, lo:hi]
-            nc.scalar.activation(out=part, in_=part, func=ACT.Silu)
+        def region(group):
+            (first, first_h), (last, last_h) = group[0], group[-1]
+            return slice(first, last + 1), slice(first_h * BANK, (last_h + 1) * BANK)
 
-        def store(first, last, lo, hi):
-            nc.sync.dma_start(out=out_tiles[:, first : last + 1, lo:hi], in_=results[:, first : last + 1, lo:hi])
+        def activate(group):
+            tiles, cols = region(group)
+            nc.scalar.activation(out=results[:, tiles, cols], in_=results[:, tiles, cols], func=ACT.Silu)
 
-        def finish_pair(n, pair):
-            (i, h), (last, last_h) = pair
-            if i < BY_BANKS_FROM:
-                parts = [(h * BANK, (last_h + 1) * BANK)]
-            else:
-                parts = [(0, BANK), (BANK, M)]
-            for lo, hi in parts:
-                activate(i, last, lo, hi)
-                store(i, last, lo, hi)
-
-        def prepare_gpsimd(c):
-            cast_gpsimd(c)
-            if c in GPSIMD_SQUARES_AFTER:
-                square_gpsimd(GPSIMD_SQUARES_AFTER[c])
+        def store(group):
+            tiles, cols = region(group)
+            nc.sync.dma_start(out=out_tiles[:, tiles, cols], in_=results[:, tiles, cols])
 
         for plane in planes:
             nc.vector.memset(plane[:].bitcast(I32), 0)
@@ -192,11 +181,10 @@ def tile_mix_feat_tm_quad_silu_kernel(tc, x, w4_words, w4_scales, w8_words, w8_s
         load_x(1)
         load_w4(0)
         load_scales(SQUARE, w4_scales)
-        for i in range(2, len(LOADS) - 2):
+        for i in range(2, len(LOADS) - 1):
             load_x(i)
         load_w8(1)
         load_w4(1)
-        load_x(len(LOADS) - 2)
         load_x(len(LOADS) - 1)
 
         spread = []
@@ -213,49 +201,57 @@ def tile_mix_feat_tm_quad_silu_kernel(tc, x, w4_words, w4_scales, w8_words, w8_s
                 spread[h][:].rearrange("q (c p) -> q p c", c=PACK),
             )
 
-        cast_vector(0)
-        square_scalar(0)
-        quantize_both(0)
+        cast_vector(0, 0, CHUNKS[0])
+        square_scalar(0, 0, CHUNKS[0])
+        quantize(0, LINEAR)
+        quantize(0, SQUARE)
         copy_bias(0)
         for feat in (LINEAR, SQUARE):
-            for i in (0, 1):
+            for i in range(CHUNKS[0] // P):
                 one_pass(i, 0, feat)
-        cast_vector(1)
-        square_vector(1)
-        square_scalar(1)
+        cast_vector(1, 0, CHUNKS[1])
+        square_two_inputs(nc.vector, 1, 0, VECTOR_SQUARES)
+        square_scalar(1, VECTOR_SQUARES, CHUNKS[1])
         copy_bias(1)
-        quantize_both(1)
+        quantize(1, LINEAR)
+        quantize(1, SQUARE)
 
-        pairs = [[(i, h), (i + 1, h)] for h in range(2) for i in (0, 2)]
-        pairs.extend([(i, 0), (i, 1)] for i in range(4, TILES))
-        banks = [bank for pair in pairs for bank in pair]
+        banks = [bank for group in STORES for bank in group]
         emptied = []
 
         def multiply_ready(c):
-            tokens = chunk_start[c] if c <= LAST else T
             for n, (i, h) in enumerate(banks):
                 free = n < OPEN_BANKS or banks[n - OPEN_BANKS] in emptied
-                if i * P >= tokens or not free:
+                if i * P >= chunk_start[c] or not free:
                     return
                 if (i, h) not in acc:
                     multiply(i, h)
 
+        def prepare_gpsimd(c):
+            cast_gpsimd(c)
+            for job in GPSIMD_SQUARES.get(c, ()):
+                square_two_inputs(nc.gpsimd, *job)
+
         chunk = 2
         prepare_gpsimd(chunk)
         multiply_ready(chunk)
-        for n, pair in enumerate(pairs):
-            for i, h in pair:
-                empty(i, h)
-                emptied.append((i, h))
+        for group in STORES:
+            waiting = []
+            for bank in group:
+                empty(*bank)
+                emptied.append(bank)
+                waiting.append(bank)
                 multiply_ready(chunk)
-                for c in SCALAR_SQUARES_AT.get(len(emptied), ()):
-                    square_scalar(c)
+                if len(emptied) in SCALAR_SQUARES:
+                    square_scalar(*SCALAR_SQUARES[len(emptied)])
                 if len(emptied) == QUANTISE_AFTER.get(chunk):
-                    if chunk + 1 in VECTOR_SQUARES:
-                        square_vector(chunk + 1)
-                    quantize_both(chunk, (SQUARE, LINEAR) if chunk == LAST else (LINEAR, SQUARE))
+                    for feat in order(chunk):
+                        quantize(chunk, feat)
                     chunk = chunk + 1
                     multiply_ready(chunk)
-                    if chunk <= LAST:
+                    if chunk < len(CHUNKS):
                         prepare_gpsimd(chunk)
-            finish_pair(n, pair)
+                if len(waiting) == SILU_BANKS or bank == group[-1]:
+                    activate(waiting)
+                    waiting = []
+            store(group)

@@ -28,14 +28,14 @@ OPEN_BANKS = 8
 LOADS = [256, 256, 128, 128, 256, 512]
 CHUNKS = [256, 256, 256, 256, 256, 128, 128]
 VECTOR_SQUARES = 48
-GPSIMD_SQUARES = {3: [(3, 128, 256), (4, 176, 256)], 4: [(4, 128, 176)], 5: [(6, 24, 128)]}
-SCALAR_SQUARES = {1: (2, 0, 256), 3: (3, 0, 128), 11: (4, 0, 128), 15: (5, 0, 128), 17: (6, 0, 24)}
-QUANTISE_AFTER = {2: 2, 3: 10, 4: 14, 5: 18, 6: 20}
-SQUARES_FIRST = (2, 6)
+GPSIMD_SQUARES = {3: [(3, 96, 256)], 4: [(4, 192, 256)], 5: [(6, 8, 128)]}
+SCALAR_SQUARES = {1: (2, 0, 256), 5: (3, 0, 96), 11: (4, 0, 192), 15: (5, 0, 128), 18: (6, 0, 8)}
+QUANTISE_AFTER = {2: 4, 3: 10, 4: 14, 5: 18, 6: 20}
+SQUARES_FIRST = (6,)
 SILU_BANKS = 1
-LOW_FIRST = 6
+LOW_FIRST = 4
 BANKS = [(i, h) for h in range(2) for i in range(LOW_FIRST)] + [(i, h) for i in range(LOW_FIRST, TILES) for h in range(2)]
-PAIRS = range(0, 14, 2)
+PAIRS = range(0, 10, 2)
 STORES = [BANKS[n : n + 2] if n in PAIRS else BANKS[n : n + 1] for n in range(len(BANKS)) if n - 1 not in PAIRS]
 
 
@@ -181,10 +181,11 @@ def tile_mix_feat_tm_quad_silu_kernel(tc, x, w4_words, w4_scales, w8_words, w8_s
         load_x(1)
         load_w4(0)
         load_scales(SQUARE, w4_scales)
-        for i in range(2, len(LOADS) - 1):
+        for i in range(2, len(LOADS) - 2):
             load_x(i)
         load_w8(1)
         load_w4(1)
+        load_x(len(LOADS) - 2)
         load_x(len(LOADS) - 1)
 
         spread = []

@@ -64,6 +64,7 @@ def tile_mix_feat_tm_quad_silu_kernel(tc, x, w4_words, w4_scales, w8_words, w8_s
         results = keep.tile([P, TILES, M], F32, name="results", align_bytes=BURST)
         out_tiles = out.rearrange("(i p) n -> p i n", p=P)
         acc = {}
+        started = []
 
         x_rows = x.rearrange("(p j) t -> p j t", j=PACK)
         w8_src = w8_words[0].rearrange("p n i -> p (n i)").bitcast(I32)
@@ -137,8 +138,9 @@ def tile_mix_feat_tm_quad_silu_kernel(tc, x, w4_words, w4_scales, w8_words, w8_s
         def one_pass(i, h, feat, first=LINEAR):
             c = chunk_of(i)
             cols = slice(i * P - chunk_start[c], (i + 1) * P - chunk_start[c])
-            if feat == first:
+            if (i, h) not in acc:
                 acc[i, h] = psum.tile([P, BANK], F32, name="acc")
+            started.append((i, h))
             nc.tensor.matmul_mx(
                 out=acc[i, h][:],
                 lhsT=codes[c][:, feat, cols].bitcast(FP8X4),
@@ -202,14 +204,27 @@ def tile_mix_feat_tm_quad_silu_kernel(tc, x, w4_words, w4_scales, w8_words, w8_s
                 spread[h][:].rearrange("q (c p) -> q p c", c=PACK),
             )
 
-        cast_vector(0, 0, CHUNKS[0])
+        cast_vector(0, 0, P)
+        cast_vector(0, P, CHUNKS[0])
         square_scalar(0, 0, CHUNKS[0])
-        quantize(0, LINEAR)
+        quantize(0, LINEAR, 0, P)
+        quantize(0, LINEAR, P)
         quantize(0, SQUARE)
         copy_bias(0)
-        for feat in (LINEAR, SQUARE):
-            for i in range(CHUNKS[0] // P):
-                one_pass(i, 0, feat)
+        for i in (0, 1):
+            one_pass(i, 0, LINEAR)
+        acc[2, 0] = psum.tile([P, BANK], F32, name="acc")
+        nc.tensor.matmul_mx(
+            out=acc[2, 0][:, 0 : BANK // 2],
+            lhsT=codes[0][:, LINEAR, 0:P].bitcast(FP8X4),
+            lhsT_scale=scales[0][:, LINEAR, 0:P],
+            rhs=w8[0][:, 0 : BANK // 2].bitcast(FP8X4),
+            rhs_scale=planes[LINEAR][:, 0 : BANK // 2],
+            start=True,
+            stop=True,
+        )
+        for i in (0, 1):
+            one_pass(i, 0, SQUARE)
         cast_vector(1, 0, CHUNKS[1])
         square_two_inputs(nc.vector, 1, 0, VECTOR_SQUARES)
         square_scalar(1, VECTOR_SQUARES, CHUNKS[1])
@@ -225,7 +240,7 @@ def tile_mix_feat_tm_quad_silu_kernel(tc, x, w4_words, w4_scales, w8_words, w8_s
                 free = n < OPEN_BANKS or banks[n - OPEN_BANKS] in emptied
                 if i * P >= chunk_start[c] or not free:
                     return
-                if (i, h) not in acc:
+                if (i, h) not in started:
                     multiply(i, h)
 
         def prepare_gpsimd(c):

@@ -213,16 +213,6 @@ def tile_mix_feat_tm_quad_silu_kernel(tc, x, w4_words, w4_scales, w8_words, w8_s
         copy_bias(0)
         for i in (0, 1):
             one_pass(i, 0, LINEAR)
-        acc[2, 0] = psum.tile([P, BANK], F32, name="acc")
-        nc.tensor.matmul_mx(
-            out=acc[2, 0][:, 0 : BANK // 2],
-            lhsT=codes[0][:, LINEAR, 0:P].bitcast(FP8X4),
-            lhsT_scale=scales[0][:, LINEAR, 0:P],
-            rhs=w8[0][:, 0 : BANK // 2].bitcast(FP8X4),
-            rhs_scale=planes[LINEAR][:, 0 : BANK // 2],
-            start=True,
-            stop=True,
-        )
         for i in (0, 1):
             one_pass(i, 0, SQUARE)
         cast_vector(1, 0, CHUNKS[1])

from contextlib import ExitStack

import concourse.mybir as mybir
from concourse.masks import make_identity

K, M, T = 512, 1024, 1536
FLOPS = 2 * 2 * K * M * T

F32 = mybir.dt.float32
BF16 = mybir.dt.bfloat16
I32 = mybir.dt.int32
U32 = mybir.dt.uint32
U8 = mybir.dt.uint8
FP8X4 = mybir.dt.float8_e4m3fn_x4
FP4X4 = mybir.dt.float4_e2m1fn_x4
ACT = mybir.ActivationFunctionType
ALU = mybir.AluOpType

P = 128
PACK = 4
BANK = 512
TILES = T // P
BURST = 256
RUN = 2
LINEAR, SQUARE = 0, 1
OPEN_BANKS = 8

LOADS = [256, 256, 128, 128, 256, 512]
CHUNKS = [256, 256, 256, 256, 256, 128, 128]
VECTOR_SQUARES = 48
GPSIMD_SQUARES = {3: [(3, 96, 256)], 4: [(4, 192, 256)], 5: [(6, 8, 128)]}
SCALAR_SQUARES = {1: (2, 0, 256), 5: (3, 0, 96), 11: (4, 0, 192), 15: (5, 0, 128), 18: (6, 0, 8)}
QUANTISE_AFTER = {2: 4, 3: 10, 4: 14, 5: 18, 6: 20}
SQUARES_FIRST = (6,)
SILU_BANKS = 1
LOW_FIRST = 4
BANKS = [(i, h) for h in range(2) for i in range(LOW_FIRST)] + [(i, h) for i in range(LOW_FIRST, TILES) for h in range(2)]
PAIRS = range(0, 10, 2)
STORES = [BANKS[n : n + 2] if n in PAIRS else BANKS[n : n + 1] for n in range(len(BANKS)) if n - 1 not in PAIRS]


def tile_mix_feat_tm_quad_silu_kernel(tc, x, w4_words, w4_scales, w8_words, w8_scales, b, out):
    nc = tc.nc
    with ExitStack() as ctx:
        keep = ctx.enter_context(tc.tile_pool(name="keep", bufs=1))
        psum = ctx.enter_context(tc.psum_pool(name="psum", bufs=OPEN_BANKS))
        ctx.enter_context(tc.manual_schedule())

        w8 = [keep.tile([P, BANK], U32, name="w8_%d" % h, align_bytes=BURST) for h in range(2)]
        w4 = [keep.tile([P, 2 * BANK], U8, name="w4_%d" % h, align_bytes=BURST) for h in range(2)]
        planes = [keep.tile([P, M], U8, name="plane%d" % f, align_bytes=BURST) for f in range(2)]
        b_cols = keep.tile([P, 2, 2 * PACK], F32, name="b_cols")
        ident = keep.tile([P, P], F32, name="ident")
        warm = keep.tile([P, 1], F32, name="warm")
        bias = keep.tile([P, M], F32, name="bias")

        load_start = [sum(LOADS[:i]) for i in range(len(LOADS))]
        raw = [keep.tile([P, PACK, w], F32, name="raw%d" % i, align_bytes=BURST) for i, w in enumerate(LOADS)]
        chunk_start = [sum(CHUNKS[:c]) for c in range(len(CHUNKS) + 1)]
        xb = keep.tile([P, max(CHUNKS) * PACK], BF16, name="xb", align_bytes=64)
        xa = [keep.tile([P, w * PACK], BF16, name="xa%d" % c, align_bytes=64) for c, w in enumerate(CHUNKS)]
        codes = [keep.tile([P, 2, w], U32, name="codes%d" % c, align_bytes=64) for c, w in enumerate(CHUNKS)]
        scales = [keep.tile([P, 2, w], U8, name="scales%d" % c, align_bytes=64) for c, w in enumerate(CHUNKS)]
        results = keep.tile([P, TILES, M], F32, name="results", align_bytes=BURST)
        out_tiles = out.rearrange("(i p) n -> p i n", p=P)
        acc = {}
        started = []

        x_rows = x.rearrange("(p j) t -> p j t", j=PACK)
        w8_src = w8_words[0].rearrange("p n i -> p (n i)").bitcast(I32)
        w4_src = w4_words[0].bitcast(I32)

        def load_x(i):
            nc.sync.dma_start(out=raw[i][:], in_=x_rows[:, :, load_start[i] : load_start[i] + LOADS[i]])

        def load_scales(feat, src):
            for r in range(4):
                nc.sync.dma_start(out=planes[feat][r:P:32, :].bitcast(I32), in_=src[0, r:16:4, :].bitcast(I32))

        def load_w8(h):
            nc.sync.dma_start(out=w8[h][:].bitcast(I32), in_=w8_src[:, h * BANK : (h + 1) * BANK])

        def load_w4(h):
            nc.sync.dma_start(out=w4[h][:].bitcast(I32), in_=w4_src[:, h * BANK // 2 : (h + 1) * BANK // 2])

        def flat(c, feat):
            return xb[:, 0 : CHUNKS[c] * PACK] if feat == LINEAR else xa[c][:]

        def raw_runs(c, lo, hi):
            i = max(j for j in range(len(LOADS)) if load_start[j] <= chunk_start[c] + lo)
            t0 = chunk_start[c] - load_start[i]
            return raw[i][:, :, t0 + lo : t0 + hi].rearrange("p j (g i) -> p g j i", i=RUN)

        def feature_runs(c, feat, lo, hi):
            words = flat(c, feat).rearrange("p (t j) -> p t j", j=PACK)
            return words[:, lo:hi, :].rearrange("p (g i) j -> p g j i", i=RUN)

        def by_load(c, lo, hi):
            cuts = [t - chunk_start[c] for t in load_start if lo < t - chunk_start[c] < hi]
            return zip([lo] + cuts, cuts + [hi])

        def cast_vector(c, lo, hi):
            nc.vector.tensor_copy(out=feature_runs(c, LINEAR, lo, hi), in_=raw_runs(c, lo, hi))

        def cast_gpsimd(c):
            for lo, hi in by_load(c, 0, CHUNKS[c]):
                nc.gpsimd.tensor_scalar(
                    out=feature_runs(c, LINEAR, lo, hi),
                    in0=raw_runs(c, lo, hi),
                    scalar1=1.0,
                    scalar2=0.0,
                    op0=ALU.mult,
                    op1=ALU.add,
                )

        def square_two_inputs(engine, c, lo, hi):
            src = raw_runs(c, lo, hi)
            engine.tensor_tensor(out=feature_runs(c, SQUARE, lo, hi), in0=src, in1=src, op=ALU.mult)

        def square_scalar(c, start, stop):
            for lo, hi in by_load(c, start, stop):
                nc.scalar.activation(out=feature_runs(c, SQUARE, lo, hi), in_=raw_runs(c, lo, hi), func=ACT.Square)

        def quantize(c, feat, lo=0, hi=None):
            cols = slice(lo, hi or CHUNKS[c])
            nc.vector.quantize_mx(
                out=codes[c][:, feat, cols].bitcast(FP8X4),
                scales=scales[c][:, feat, cols],
                in_=flat(c, feat)[:, cols.start * PACK : cols.stop * PACK],
            )

        def chunk_of(i):
            return max(j for j in range(len(CHUNKS)) if chunk_start[j] <= i * P)

        def order(c):
            return (SQUARE, LINEAR) if c in SQUARES_FIRST else (LINEAR, SQUARE)

        def one_pass(i, h, feat, first=LINEAR):
            c = chunk_of(i)
            cols = slice(i * P - chunk_start[c], (i + 1) * P - chunk_start[c])
            if (i, h) not in acc:
                acc[i, h] = psum.tile([P, BANK], F32, name="acc")
            started.append((i, h))
            nc.tensor.matmul_mx(
                out=acc[i, h][:],
                lhsT=codes[c][:, feat, cols].bitcast(FP8X4),
                lhsT_scale=scales[c][:, feat, cols],
                rhs=w8[h][:].bitcast(FP8X4) if feat == LINEAR else w4[h][:].bitcast(FP4X4),
                rhs_scale=planes[feat][:, h * BANK : (h + 1) * BANK],
                start=feat == first,
                stop=feat != first,
            )

        def multiply(i, h):
            first, second = order(chunk_of(i))
            one_pass(i, h, first, first)
            one_pass(i, h, second, first)

        def empty(i, h):
            n = slice(h * BANK, (h + 1) * BANK)
            nc.vector.tensor_tensor(out=results[:, i, n], in0=acc[i, h][:], in1=bias[:, n], op=ALU.add)

        def region(group):
            (first, first_h), (last, last_h) = group[0], group[-1]
            return slice(first, last + 1), slice(first_h * BANK, (last_h + 1) * BANK)

        def activate(group):
            tiles, cols = region(group)
            nc.scalar.activation(out=results[:, tiles, cols], in_=results[:, tiles, cols], func=ACT.Silu)

        def store(group):
            tiles, cols = region(group)
            nc.sync.dma_start(out=out_tiles[:, tiles, cols], in_=results[:, tiles, cols])

        for plane in planes:
            nc.vector.memset(plane[:].bitcast(I32), 0)
        nc.sync.dma_start(out=b_cols[:, :, 0:PACK], in_=b.rearrange("(h p c) -> p h c", h=2, c=PACK))
        load_x(0)
        make_identity(nc, ident[:])
        load_scales(LINEAR, w8_scales)
        nc.scalar.activation(out=warm[:], in_=ident[:, 0:1], func=ACT.Silu)
        load_w8(0)
        load_x(1)
        load_w4(0)
        load_scales(SQUARE, w4_scales)
        for i in range(2, len(LOADS) - 2):
            load_x(i)
        load_w8(1)
        load_w4(1)
        load_x(len(LOADS) - 2)
        load_x(len(LOADS) - 1)

        spread = []
        for h in range(2):
            bank = psum.tile([P, BANK], F32, name="acc")
            for c in range(PACK):
                col = b_cols[:, h, c : c + 1]
                nc.tensor.transpose(bank[:, c * P : (c + 1) * P], col.to_broadcast([P, P]), ident[:])
            spread.append(bank)

        def copy_bias(h):
            nc.scalar.copy(
                bias[:, h * BANK : (h + 1) * BANK].rearrange("q (p c) -> q p c", c=PACK),
                spread[h][:].rearrange("q (c p) -> q p c", c=PACK),
            )

        cast_vector(0, 0, P)
        cast_vector(0, P, CHUNKS[0])
        square_scalar(0, 0, CHUNKS[0])
        quantize(0, LINEAR, 0, P)
        quantize(0, LINEAR, P)
        quantize(0, SQUARE)
        copy_bias(0)
        for i in (0, 1):
            one_pass(i, 0, LINEAR)
        for i in (0, 1):
            one_pass(i, 0, SQUARE)
        cast_vector(1, 0, CHUNKS[1])
        square_two_inputs(nc.vector, 1, 0, VECTOR_SQUARES)
        square_scalar(1, VECTOR_SQUARES, CHUNKS[1])
        copy_bias(1)
        quantize(1, LINEAR)
        quantize(1, SQUARE)

        banks = [bank for group in STORES for bank in group]
        emptied = []

        def multiply_ready(c):
            for n, (i, h) in enumerate(banks):
                free = n < OPEN_BANKS or banks[n - OPEN_BANKS] in emptied
                if i * P >= chunk_start[c] or not free:
                    return
                if (i, h) not in started:
                    multiply(i, h)

        def prepare_gpsimd(c):
            cast_gpsimd(c)
            for job in GPSIMD_SQUARES.get(c, ()):
                square_two_inputs(nc.gpsimd, *job)

        chunk = 2
        prepare_gpsimd(chunk)
        multiply_ready(chunk)
        for group in STORES:
            waiting = []
            for bank in group:
                empty(*bank)
                emptied.append(bank)
                waiting.append(bank)
                multiply_ready(chunk)
                if len(emptied) in SCALAR_SQUARES:
                    square_scalar(*SCALAR_SQUARES[len(emptied)])
                if len(emptied) == QUANTISE_AFTER.get(chunk):
                    for feat in order(chunk):
                        quantize(chunk, feat)
                    chunk = chunk + 1
                    multiply_ready(chunk)
                    if chunk < len(CHUNKS):
                        prepare_gpsimd(chunk)
                if len(waiting) == SILU_BANKS or bank == group[-1]:
                    activate(waiting)
                    waiting = []
            store(group)
